import numpy as np
import ml_dtypes


def mxq(x, axis, fmt="e4m3"):
    dtype, down = {"e4m3": (ml_dtypes.float8_e4m3fn, 7), "e5m2": (ml_dtypes.float8_e5m2, 14)}[fmt]
    v = np.moveaxis(np.asarray(x, np.float32).astype(ml_dtypes.bfloat16).astype(np.float64), axis, -1)
    blocks = v.reshape(v.shape[:-1] + (-1, 32))
    amax = np.abs(blocks).max(-1, keepdims=True)
    byte = np.maximum(np.where(amax > 0, np.frexp(amax)[1] - 1 + 127, 0) - down, 1)
    scale = np.exp2(byte - 127.0)
    codes = (blocks / scale).astype(np.float32).astype(dtype).astype(np.float64)
    return np.moveaxis((codes * scale).reshape(v.shape), -1, axis)


WIDE = False


def mx_kscale(k):
    if not WIDE:
        return np.ones(k)
    levels = np.array([10, -10, 5, -5, 0])
    if k % 512:
        return np.exp2(np.random.permutation(np.resize(levels, k // 32))).repeat(32)
    a = np.empty((k // 512, 16))
    for p in range(k // 512):
        a[p, :8] = np.random.permutation(np.resize(levels, 8))
        for g in range(8):
            far = levels[np.abs(levels - a[p, g]) >= 10]
            a[p, g + 8] = far[np.random.randint(len(far))]
    return np.exp2(a.ravel()).repeat(32)


def f64(x):
    return np.asarray(x).astype(np.float64)


def striped(idx):
    return np.tile(idx.reshape(-1, 16).T, (8, 1)).astype(np.uint16)


def unstriped(offs):
    return offs[:16].T.reshape(-1).astype(np.int64)


def pack_weight(w):
    k, n = w.shape
    w = f64(np.asarray(w, np.float32).astype(ml_dtypes.bfloat16)).reshape(k // 32, 32, n)
    amax = np.abs(w).max(1)
    byte = np.clip(np.where(amax > 0, np.frexp(amax)[1] - 1 + 127 - 7, 1), 1, 254)
    scaled = (w * np.exp2(127.0 - byte)[:, None, :]).reshape(k, n).astype(np.float32)
    words = np.ascontiguousarray(scaled.reshape(k // 512, 128, 4, n).transpose(0, 1, 3, 2)).astype(ml_dtypes.float8_e4m3fn).view(np.uint8)
    return words, np.ascontiguousarray(byte.astype(np.uint8).reshape(k // 512, 16, n))


def unpack_weight(words, scales):
    g, p, n, _ = words.shape
    vals = np.ascontiguousarray(words).view(ml_dtypes.float8_e4m3fn).astype(np.float64) * np.repeat(np.exp2(scales.astype(np.float64) - 127.0), 8, axis=1)[..., None]
    return vals.transpose(0, 1, 3, 2).reshape(g * 512, n)


def sigmoid(v):
    return 1.0 / (1.0 + np.exp(-np.maximum(v, -700.0)))


def gelu(v):
    return 0.5 * v * (1.0 + np.tanh(np.sqrt(2.0 / np.pi) * (v + 0.044715 * v**3)))


K, T, S, N = 1024, 1024, 512, 256


def setup_inputs():
    n = np.random.standard_normal
    s = mx_kscale(K)[:, None]
    packed_w1 = pack_weight(n((K, N)) / np.sqrt(K) / s)
    packed_w2 = pack_weight(n((K, N)) / np.sqrt(K) / s)
    return {
        "xT": (n((K, T)) * s).astype(np.float32),
        "res": n((N, T)).astype(np.float32),
        "w1_words": packed_w1[0],
        "w1_scales": packed_w1[1],
        "w2_words": packed_w2[0],
        "w2_scales": packed_w2[1],
        "offs": striped(np.random.permutation(T)[:S]),
    }


def reference(xT, res, w1_words, w1_scales, w2_words, w2_scales, offs):
    r = f64(res)[:, unstriped(offs)]
    xq = mxq(f64(xT)[:, unstriped(offs)], 0, "e4m3")
    g = sigmoid(unpack_weight(w2_words, w2_scales).T @ xq)
    y = gelu(unpack_weight(w1_words, w1_scales).T @ xq)
    return r + g * (y - r)

@@ -1,0 +1,174 @@
+from contextlib import ExitStack
+
+import concourse.mybir as mybir
+
+K, T, S, N = 1024, 1024, 512, 256
+FLOPS = 2 * 2 * K * N * S
+
+F32 = mybir.dt.float32
+BF16 = mybir.dt.bfloat16
+I32 = mybir.dt.int32
+U32 = mybir.dt.uint32
+U16 = mybir.dt.uint16
+U8 = mybir.dt.uint8
+FP8X4 = mybir.dt.float8_e4m3fn_x4
+ACT = mybir.ActivationFunctionType
+ALU = mybir.AluOpType
+
+P = 128
+PASSES = K // 512
+HALF = S // 2
+M_TILES = N // P
+
+
+def tile_picked_highway_gelu_l_kernel(
+    tc, xT, res, w1_words, w1_scales, w2_words, w2_scales, offs, out
+):
+    nc = tc.nc
+    with ExitStack() as ctx:
+        keep = ctx.enter_context(tc.tile_pool(name="keep", bufs=1))
+        psum = ctx.enter_context(tc.psum_pool(name="psum", bufs=1))
+
+        offsets = keep.tile([P, S // 16], U16, name="offsets")
+        half_offsets = [offsets[:, h * (HALF // 16) : (h + 1) * (HALF // 16)] for h in range(2)]
+
+        x_rows = xT.rearrange("(g p u e) c -> g u p e c", g=PASSES, p=P, u=2, e=2)
+        pieces = {(0, 0): [(0, T)], (0, 1): [(0, T)], (1, 0): [(0, T)], (1, 1): [(0, T // 2), (T // 2, T)]}
+        w_planes = keep.tile([P, N], U8, name="w_planes", align_bytes=64)
+        nc.gpsimd.memset(w_planes[:].bitcast(I32), 0)
+
+        def load_scales(i, scales):
+            for q in range(4):
+                row0 = 32 * q + 8 * i
+                nc.sync.dma_start(
+                    out=w_planes[row0 : row0 + 8, :].bitcast(I32),
+                    in_=scales[:, 4 * q : 4 * q + 4, :].bitcast(I32),
+                )
+
+        raw = {}
+        for g in range(PASSES):
+            for u in range(2):
+                for c0, c1 in pieces[g, u]:
+                    raw[g, u, c0] = keep.tile([P, 2, c1 - c0], F32, name=f"raw{g}{u}_{c0}", tag=f"raw{g}{u}_{c0}", align_bytes=64)
+                    nc.sync.dma_start(out=raw[g, u, c0][:], in_=x_rows[g, u, :, :, c0:c1])
+                if (g, u) == (0, 0):
+                    nc.sync.dma_start(offsets[:], offs)
+                if (g, u) == (0, 1):
+                    load_scales(0, w1_scales)
+                if (g, u) == (1, 1):
+                    load_scales(1, w2_scales)
+
+        w_codes = []
+        for i, words in enumerate((w1_words, w2_words)):
+            codes = keep.tile([P, PASSES, N], U32, name=f"w_codes{i}", align_bytes=64)
+            nc.sync.dma_start(
+                out=codes[:].bitcast(I32),
+                in_=words.rearrange("g p n t -> p g (n t)").bitcast(I32),
+            )
+            w_codes.append(codes)
+
+        res_rows = []
+        for m in range(M_TILES):
+            rows = keep.tile([P, T], F32, name=f"res{m}")
+            nc.sync.dma_start(out=rows[:], in_=res[m * P : (m + 1) * P, :])
+            res_rows.append(rows)
+
+        zero_in = keep.tile([P, 1], F32, name="zero_in")
+        zero_bias = keep.tile([P, 1], F32, name="zero_bias")
+        nc.vector.memset(zero_in[:], 0.0)
+        nc.scalar.activation(out=zero_bias[:], in_=zero_in[:], func=ACT.Gelu_apprx_tanh)
+
+        vector_cols = {(0, 0, 0): 704, (0, 1, 0): 608, (1, 0, 0): 1024, (1, 1, 0): 0, (1, 1, 512): 0}
+        x_codes, x_planes, pairs, picked = {}, {}, {}, {}
+
+        def cast(g, u):
+            pairs[g, u] = keep.tile([P, T], U32, name=f"pairs{g}{u}")
+            pairs_bf = pairs[g, u][:].bitcast(BF16).rearrange("p (c e) -> p c e", e=2)
+            for c0, c1 in pieces[g, u]:
+                source = raw[g, u, c0][:].rearrange("p e c -> p c e")
+                cut = vector_cols[g, u, c0]
+                if cut < c1 - c0:
+                    nc.scalar.copy(out=pairs_bf[:, c0 + cut : c1, :], in_=source[:, cut:, :])
+                if cut:
+                    nc.vector.tensor_copy(out=pairs_bf[:, c0 : c0 + cut, :], in_=source[:, :cut, :])
+
+        def gather(g, u):
+            for h in range(2):
+                if u == 0:
+                    picked[g, h] = keep.tile([P, 2, HALF], U32, name=f"picked{g}{h}")
+                nc.vector.tensor_copy(picked[g, h][:, u, :], pairs[g, u][:].indirect(half_offsets[h]))
+
+        woven = {}
+
+        def weave(g):
+            for h in range(2):
+                woven[g, h] = keep.tile([P, 2 * HALF], U32, name=f"woven{g}{h}", align_bytes=64)
+                nc.scalar.copy(
+                    out=woven[g, h][:].rearrange("p (j u) -> p j u", u=2),
+                    in_=picked[g, h][:].rearrange("p u j -> p j u"),
+                )
+
+        def quantise(g, tag):
+            codes = keep.tile([P, S], U32, name=f"x_codes{g}", tag=tag, align_bytes=64)
+            for h in range(2):
+                x_codes[g, h] = codes[:, h * HALF : (h + 1) * HALF]
+                x_planes[g, h] = keep.tile([P, HALF], U8, name=f"x_planes{g}{h}", align_bytes=64)
+                nc.vector.quantize_mx(
+                    out=x_codes[g, h].bitcast(FP8X4),
+                    scales=x_planes[g, h][:],
+                    in_=woven[g, h][:].bitcast(BF16),
+                )
+
+        cast(0, 0)
+        gather(0, 0)
+        cast(0, 1)
+        gather(0, 1)
+        weave(0)
+        cast(1, 0)
+        quantise(0, "raw10_0")
+        gather(1, 0)
+        cast(1, 1)
+        gather(1, 1)
+        weave(1)
+        quantise(1, "x_codes1")
+
+        passing = {}
+        for h in range(2):
+            passing[h] = keep.tile([P, HALF], F32, name=f"passing{h}")
+            nc.vector.tensor_copy(passing[h][:], res_rows[0][:].indirect(half_offsets[h]))
+
+        for h in range(2):
+            sums = {}
+            for g in range(PASSES):
+                for m in range(M_TILES):
+                    for i in range(2):
+                        if g == 0:
+                            sums[i, m] = psum.tile([P, HALF], F32, name=f"sum{h}{i}{m}")
+                        cols = slice(m * P, (m + 1) * P)
+                        nc.tensor.matmul_mx(
+                            out=sums[i, m][:],
+                            lhsT=w_codes[i][:, g, cols].bitcast(FP8X4),
+                            lhsT_scale=w_planes[8 * i + 4 * g :, cols],
+                            rhs=x_codes[g, h].bitcast(FP8X4),
+                            rhs_scale=x_planes[g, h][:],
+                            start=(g == 0),
+                            stop=(g == PASSES - 1),
+                        )
+            y, th, d = {}, {}, {}
+            for m in range(M_TILES):
+                y[m] = keep.tile([P, HALF], F32, name=f"y{h}{m}")
+                th[m] = keep.tile([P, HALF], F32, name=f"th{h}{m}")
+                nc.scalar.activation(out=y[m][:], in_=sums[0, m][:], func=ACT.Gelu_apprx_tanh, bias=zero_bias[:])
+                nc.scalar.activation(out=th[m][:], in_=sums[1, m][:], func=ACT.Tanh, bias=zero_bias[:], scale=0.5)
+            for m in range(M_TILES):
+                d[m] = keep.tile([P, HALF], F32, name=f"d{h}{m}")
+                r = passing[h][:] if m == 0 else res_rows[m][:].indirect(half_offsets[h])
+                nc.vector.tensor_tensor(d[m][:], r, y[m][:], ALU.subtract)
+            e = {}
+            for m in range(M_TILES):
+                e[m] = keep.tile([P, HALF], F32, name=f"e{h}{m}")
+                nc.vector.scalar_tensor_tensor(e[m][:], th[m][:], 1.0, d[m][:], ALU.subtract, ALU.mult)
+            for m in range(M_TILES):
+                o = keep.tile([P, HALF], F32, name=f"o{h}{m}")
+                nc.vector.scalar_tensor_tensor(o[:], e[m][:], -0.5, y[m][:], ALU.mult, ALU.add)
+                nc.sync.dma_start(out=out[m * P : (m + 1) * P, h * HALF : (h + 1) * HALF], in_=o[:])

@@ -33,18 +33,19 @@ def tile_picked_highway_gelu_l_kernel(
         half_offsets = [offsets[:, h * (HALF // 16) : (h + 1) * (HALF // 16)] for h in range(2)]
 
         x_rows = xT.rearrange("(g p u e) c -> g u p e c", g=PASSES, p=P, u=2, e=2)
-        pieces = {(0, 0): [(0, T)], (0, 1): [(0, T)], (1, 0): [(0, T)], (1, 1): [(0, T // 2), (T // 2, T)]}
+        pieces = {(0, 0): [(0, T // 2), (T // 2, T)], (0, 1): [(0, T)], (1, 0): [(0, T)], (1, 1): [(0, T // 2), (T // 2, T)]}
         w_planes = keep.tile([P, N], U8, name="w_planes", align_bytes=64)
         nc.gpsimd.memset(w_planes[:].bitcast(I32), 0)
 
-        def load_scales(i, scales):
+        def load_scales(queue, i, scales):
             for q in range(4):
                 row0 = 32 * q + 8 * i
-                nc.sync.dma_start(
+                queue.dma_start(
                     out=w_planes[row0 : row0 + 8, :].bitcast(I32),
                     in_=scales[:, 4 * q : 4 * q + 4, :].bitcast(I32),
                 )
 
+        load_scales(nc.gpsimd, 1, w2_scales)
         raw = {}
         for g in range(PASSES):
             for u in range(2):
@@ -54,18 +55,16 @@ def tile_picked_highway_gelu_l_kernel(
                 if (g, u) == (0, 0):
                     nc.sync.dma_start(offsets[:], offs)
                 if (g, u) == (0, 1):
-                    load_scales(0, w1_scales)
-                if (g, u) == (1, 1):
-                    load_scales(1, w2_scales)
+                    load_scales(nc.sync, 0, w1_scales)
 
-        w_codes = []
-        for i, words in enumerate((w1_words, w2_words)):
-            codes = keep.tile([P, PASSES, N], U32, name=f"w_codes{i}", align_bytes=64)
-            nc.sync.dma_start(
-                out=codes[:].bitcast(I32),
-                in_=words.rearrange("g p n t -> p g (n t)").bitcast(I32),
-            )
-            w_codes.append(codes)
+        w_codes = {}
+        for g in range(PASSES):
+            for i, words in enumerate((w1_words, w2_words)):
+                w_codes[i, g] = keep.tile([P, N], U32, name=f"w_codes{i}{g}", align_bytes=64)
+                nc.sync.dma_start(
+                    out=w_codes[i, g][:].bitcast(I32),
+                    in_=words[g].rearrange("p n t -> p (n t)").bitcast(I32),
+                )
 
         res_rows = []
         for m in range(M_TILES):
@@ -78,7 +77,7 @@ def tile_picked_highway_gelu_l_kernel(
         nc.vector.memset(zero_in[:], 0.0)
         nc.scalar.activation(out=zero_bias[:], in_=zero_in[:], func=ACT.Gelu_apprx_tanh)
 
-        vector_cols = {(0, 0, 0): 704, (0, 1, 0): 608, (1, 0, 0): 1024, (1, 1, 0): 0, (1, 1, 512): 0}
+        vector_cols = {(0, 0, 0): 0, (0, 0, 512): 352, (0, 1, 0): 704, (1, 0, 0): 1024, (1, 1, 0): 0, (1, 1, 512): 0}
         x_codes, x_planes, pairs, picked = {}, {}, {}, {}
 
         def cast(g, u):
@@ -102,7 +101,7 @@ def tile_picked_highway_gelu_l_kernel(
 
         def weave(g):
             for h in range(2):
-                woven[g, h] = keep.tile([P, 2 * HALF], U32, name=f"woven{g}{h}", align_bytes=64)
+                woven[g, h] = keep.tile([P, 2 * HALF], U32, name=f"woven{g}{h}", tag=f"woven{g}{h}", align_bytes=64)
                 nc.scalar.copy(
                     out=woven[g, h][:].rearrange("p (j u) -> p j u", u=2),
                     in_=picked[g, h][:].rearrange("p u j -> p j u"),
@@ -132,43 +131,49 @@ def tile_picked_highway_gelu_l_kernel(
         weave(1)
         quantise(1, "x_codes1")
 
-        passing = {}
+        passing = [
+            keep.tile([P, HALF], F32, name="passing0"),
+            keep.tile([P, HALF], F32, name="passing1", tag="woven11", align_bytes=64),
+        ]
         for h in range(2):
-            passing[h] = keep.tile([P, HALF], F32, name=f"passing{h}")
             nc.vector.tensor_copy(passing[h][:], res_rows[0][:].indirect(half_offsets[h]))
 
-        for h in range(2):
-            sums = {}
-            for g in range(PASSES):
-                for m in range(M_TILES):
-                    for i in range(2):
+        sums = {}
+        for g in range(PASSES):
+            for i in range(2):
+                for h in range(2):
+                    for m in range(M_TILES):
                         if g == 0:
-                            sums[i, m] = psum.tile([P, HALF], F32, name=f"sum{h}{i}{m}")
+                            sums[h, i, m] = psum.tile([P, HALF], F32, name=f"sum{h}{i}{m}")
                         cols = slice(m * P, (m + 1) * P)
                         nc.tensor.matmul_mx(
-                            out=sums[i, m][:],
-                            lhsT=w_codes[i][:, g, cols].bitcast(FP8X4),
+                            out=sums[h, i, m][:],
+                            lhsT=w_codes[i, g][:, cols].bitcast(FP8X4),
                             lhsT_scale=w_planes[8 * i + 4 * g :, cols],
                             rhs=x_codes[g, h].bitcast(FP8X4),
                             rhs_scale=x_planes[g, h][:],
                             start=(g == 0),
                             stop=(g == PASSES - 1),
                         )
-            y, th, d = {}, {}, {}
+        y = [keep.tile([P, S], F32, name=f"y{m}") for m in range(M_TILES)]
+        th = [keep.tile([P, S], F32, name=f"th{m}") for m in range(M_TILES)]
+        d = [keep.tile([P, S], F32, name=f"d{m}") for m in range(M_TILES)]
+        e = [keep.tile([P, S], F32, name=f"e{m}") for m in range(M_TILES)]
+        o = [keep.tile([P, S], F32, name=f"o{m}") for m in range(M_TILES)]
+        for h in range(2):
+            cols = slice(h * HALF, (h + 1) * HALF)
             for m in range(M_TILES):
-                y[m] = keep.tile([P, HALF], F32, name=f"y{h}{m}")
-                th[m] = keep.tile([P, HALF], F32, name=f"th{h}{m}")
-                nc.scalar.activation(out=y[m][:], in_=sums[0, m][:], func=ACT.Gelu_apprx_tanh, bias=zero_bias[:])
-                nc.scalar.activation(out=th[m][:], in_=sums[1, m][:], func=ACT.Tanh, bias=zero_bias[:], scale=0.5)
-            for m in range(M_TILES):
-                d[m] = keep.tile([P, HALF], F32, name=f"d{h}{m}")
-                r = passing[h][:] if m == 0 else res_rows[m][:].indirect(half_offsets[h])
-                nc.vector.tensor_tensor(d[m][:], r, y[m][:], ALU.subtract)
-            e = {}
-            for m in range(M_TILES):
-                e[m] = keep.tile([P, HALF], F32, name=f"e{h}{m}")
-                nc.vector.scalar_tensor_tensor(e[m][:], th[m][:], 1.0, d[m][:], ALU.subtract, ALU.mult)
-            for m in range(M_TILES):
-                o = keep.tile([P, HALF], F32, name=f"o{h}{m}")
-                nc.vector.scalar_tensor_tensor(o[:], e[m][:], -0.5, y[m][:], ALU.mult, ALU.add)
-                nc.sync.dma_start(out=out[m * P : (m + 1) * P, h * HALF : (h + 1) * HALF], in_=o[:])
+                nc.scalar.activation(out=y[m][:, cols], in_=sums[h, 0, m][:], func=ACT.Gelu_apprx_tanh, bias=zero_bias[:])
+        for m in range(M_TILES):
+            for h in range(2):
+                cols = slice(h * HALF, (h + 1) * HALF)
+                nc.scalar.activation(out=th[m][:, cols], in_=sums[h, 1, m][:], func=ACT.Tanh, bias=zero_bias[:], scale=0.5)
+        for h in range(2):
+            cols = slice(h * HALF, (h + 1) * HALF)
+            nc.vector.tensor_tensor(d[0][:, cols], passing[h][:], y[0][:, cols], ALU.subtract)
+        nc.vector.tensor_tensor(d[1][:], res_rows[1][:].indirect(offsets[:]), y[1][:], ALU.subtract)
+        for m in range(M_TILES):
+            nc.vector.scalar_tensor_tensor(e[m][:], th[m][:], 1.0, d[m][:], ALU.subtract, ALU.mult)
+        for m, cols in ((0, slice(0, S)), (1, slice(0, HALF)), (1, slice(HALF, S))):
+            nc.vector.scalar_tensor_tensor(o[m][:, cols], e[m][:, cols], -0.5, y[m][:, cols], ALU.mult, ALU.add)
+            nc.sync.dma_start(out=out[m * P : (m + 1) * P, cols], in_=o[m][:, cols])

@@ -34,18 +34,15 @@ def tile_picked_highway_gelu_l_kernel(
 
         x_rows = xT.rearrange("(g p u e) c -> g u p e c", g=PASSES, p=P, u=2, e=2)
         pieces = {(0, 0): [(0, T // 2), (T // 2, T)], (0, 1): [(0, T)], (1, 0): [(0, T)], (1, 1): [(0, T // 2), (T // 2, T)]}
-        w_planes = keep.tile([P, N], U8, name="w_planes", align_bytes=64)
-        nc.gpsimd.memset(w_planes[:].bitcast(I32), 0)
+        w_planes = []
+        for i, (scales, queue) in enumerate(((w1_scales, nc.scalar), (w2_scales, nc.gpsimd))):
+            plane = keep.tile([P, PASSES, N], U8, name=f"w_planes{i}", align_bytes=64)
+            nc.gpsimd.memset(plane[:].bitcast(I32), 0)
+            by_row = scales.rearrange("g (q r) n -> r q g n", r=4)
+            for r in range(4):
+                queue.dma_start(out=plane[r:P:32, :, :].bitcast(I32), in_=by_row[r].bitcast(I32))
+            w_planes.append(plane)
 
-        def load_scales(queue, i, scales):
-            for q in range(4):
-                row0 = 32 * q + 8 * i
-                queue.dma_start(
-                    out=w_planes[row0 : row0 + 8, :].bitcast(I32),
-                    in_=scales[:, 4 * q : 4 * q + 4, :].bitcast(I32),
-                )
-
-        load_scales(nc.gpsimd, 1, w2_scales)
         raw = {}
         for g in range(PASSES):
             for u in range(2):
@@ -54,8 +51,6 @@ def tile_picked_highway_gelu_l_kernel(
                     nc.sync.dma_start(out=raw[g, u, c0][:], in_=x_rows[g, u, :, :, c0:c1])
                 if (g, u) == (0, 0):
                     nc.sync.dma_start(offsets[:], offs)
-                if (g, u) == (0, 1):
-                    load_scales(nc.sync, 0, w1_scales)
 
         w_codes = {}
         for g in range(PASSES):
@@ -149,7 +144,7 @@ def tile_picked_highway_gelu_l_kernel(
                         nc.tensor.matmul_mx(
                             out=sums[h, i, m][:],
                             lhsT=w_codes[i, g][:, cols].bitcast(FP8X4),
-                            lhsT_scale=w_planes[8 * i + 4 * g :, cols],
+                            lhsT_scale=w_planes[i][:, g, cols],
                             rhs=x_codes[g, h].bitcast(FP8X4),
                             rhs_scale=x_planes[g, h][:],
                             start=(g == 0),
@@ -172,8 +167,17 @@ def tile_picked_highway_gelu_l_kernel(
             cols = slice(h * HALF, (h + 1) * HALF)
             nc.vector.tensor_tensor(d[0][:, cols], passing[h][:], y[0][:, cols], ALU.subtract)
         nc.vector.tensor_tensor(d[1][:], res_rows[1][:].indirect(offsets[:]), y[1][:], ALU.subtract)
-        for m in range(M_TILES):
-            nc.vector.scalar_tensor_tensor(e[m][:], th[m][:], 1.0, d[m][:], ALU.subtract, ALU.mult)
-        for m, cols in ((0, slice(0, S)), (1, slice(0, HALF)), (1, slice(HALF, S))):
+
+        def gate(m, cols):
+            nc.vector.scalar_tensor_tensor(e[m][:, cols], th[m][:, cols], 1.0, d[m][:, cols], ALU.subtract, ALU.mult)
+
+        def finish(m, cols):
             nc.vector.scalar_tensor_tensor(o[m][:, cols], e[m][:, cols], -0.5, y[m][:, cols], ALU.mult, ALU.add)
             nc.sync.dma_start(out=out[m * P : (m + 1) * P, cols], in_=o[m][:, cols])
+
+        gate(0, slice(0, S))
+        gate(1, slice(0, HALF))
+        finish(0, slice(0, S))
+        gate(1, slice(HALF, S))
+        finish(1, slice(0, HALF))
+        finish(1, slice(HALF, S))

@@ -52,6 +52,12 @@ def tile_picked_highway_gelu_l_kernel(
                 if (g, u) == (0, 0):
                     nc.sync.dma_start(offsets[:], offs)
 
+        res_rows = [keep.tile([P, T], F32, name=f"res{m}") for m in range(M_TILES)]
+
+        def load_res(m):
+            nc.sync.dma_start(out=res_rows[m][:], in_=res[m * P : (m + 1) * P, :])
+
+        load_res(0)
         w_codes = {}
         for g in range(PASSES):
             for i, words in enumerate((w1_words, w2_words)):
@@ -61,18 +67,14 @@ def tile_picked_highway_gelu_l_kernel(
                     in_=words[g].rearrange("p n t -> p (n t)").bitcast(I32),
                 )
 
-        res_rows = []
-        for m in range(M_TILES):
-            rows = keep.tile([P, T], F32, name=f"res{m}")
-            nc.sync.dma_start(out=rows[:], in_=res[m * P : (m + 1) * P, :])
-            res_rows.append(rows)
+        load_res(1)
 
         zero_in = keep.tile([P, 1], F32, name="zero_in")
         zero_bias = keep.tile([P, 1], F32, name="zero_bias")
         nc.vector.memset(zero_in[:], 0.0)
         nc.scalar.activation(out=zero_bias[:], in_=zero_in[:], func=ACT.Gelu_apprx_tanh)
 
-        vector_cols = {(0, 0, 0): 0, (0, 0, 512): 352, (0, 1, 0): 704, (1, 0, 0): 1024, (1, 1, 0): 0, (1, 1, 512): 0}
+        vector_cols = {(0, 0, 0): 0, (0, 0, 512): 352, (0, 1, 0): 704, (1, 0, 0): 1024, (1, 1, 0): 0, (1, 1, 512): 288}
         x_codes, x_planes, pairs, picked = {}, {}, {}, {}
 
         def cast(g, u):
@@ -86,10 +88,11 @@ def tile_picked_highway_gelu_l_kernel(
                 if cut:
                     nc.vector.tensor_copy(out=pairs_bf[:, c0 : c0 + cut, :], in_=source[:, :cut, :])
 
-        def gather(g, u):
-            for h in range(2):
+        def gather(g, u, halves=(0, 1)):
+            for h in halves:
                 if u == 0:
-                    picked[g, h] = keep.tile([P, 2, HALF], U32, name=f"picked{g}{h}")
+                    tag = "raw11_0" if (g, h) == (1, 1) else f"picked{g}{h}"
+                    picked[g, h] = keep.tile([P, 2, HALF], U32, name=f"picked{g}{h}", tag=tag, align_bytes=64)
                 nc.vector.tensor_copy(picked[g, h][:, u, :], pairs[g, u][:].indirect(half_offsets[h]))
 
         woven = {}
@@ -120,8 +123,9 @@ def tile_picked_highway_gelu_l_kernel(
         weave(0)
         cast(1, 0)
         quantise(0, "raw10_0")
-        gather(1, 0)
+        gather(1, 0, (0,))
         cast(1, 1)
+        gather(1, 0, (1,))
         gather(1, 1)
         weave(1)
         quantise(1, "x_codes1")

@@ -16,7 +16,8 @@ ACT = mybir.ActivationFunctionType
 ALU = mybir.AluOpType
 
 P = 128
-PASSES = K // 512
+PACK = 4
+PASSES = K // (P * PACK)
 HALF = S // 2
 M_TILES = N // P
 
@@ -30,36 +31,27 @@ def tile_picked_highway_gelu_l_kernel(
         psum = ctx.enter_context(tc.psum_pool(name="psum", bufs=1))
 
         offsets = keep.tile([P, S // 16], U16, name="offsets")
+        halves = [slice(h * HALF, (h + 1) * HALF) for h in range(2)]
         half_offsets = [offsets[:, h * (HALF // 16) : (h + 1) * (HALF // 16)] for h in range(2)]
 
-        x_rows = xT.rearrange("(g p u e) c -> g u p e c", g=PASSES, p=P, u=2, e=2)
-        pieces = {(0, 0): [(0, T // 2), (T // 2, T)], (0, 1): [(0, T)], (1, 0): [(0, T)], (1, 1): [(0, T // 2), (T // 2, T)]}
+        x_rows = xT.rearrange("(g p t) c -> g t p c", g=PASSES, p=P, t=PACK)
         w_planes = []
-        for i, (scales, queue) in enumerate(((w1_scales, nc.scalar), (w2_scales, nc.gpsimd))):
+        for i in range(2):
             plane = keep.tile([P, PASSES, N], U8, name=f"w_planes{i}", align_bytes=64)
-            nc.gpsimd.memset(plane[:].bitcast(I32), 0)
-            by_row = scales.rearrange("g (q r) n -> r q g n", r=4)
-            for r in range(4):
-                queue.dma_start(out=plane[r:P:32, :, :].bitcast(I32), in_=by_row[r].bitcast(I32))
+            nc.vector.memset(plane[:].bitcast(I32), 0)
             w_planes.append(plane)
 
-        raw = {}
-        for g in range(PASSES):
-            for u in range(2):
-                for c0, c1 in pieces[g, u]:
-                    raw[g, u, c0] = keep.tile([P, 2, c1 - c0], F32, name=f"raw{g}{u}_{c0}", tag=f"raw{g}{u}_{c0}", align_bytes=64)
-                    nc.sync.dma_start(out=raw[g, u, c0][:], in_=x_rows[g, u, :, :, c0:c1])
-                if (g, u) == (0, 0):
-                    nc.sync.dma_start(offsets[:], offs)
+        rows, w_codes, res_rows = {}, {}, {}
 
-        res_rows = [keep.tile([P, T], F32, name=f"res{m}") for m in range(M_TILES)]
+        def load_x(g, t):
+            rows[g, t] = keep.tile([P, T], F32, name=f"rows{g}{t}", tag=f"rows{g}{t}", align_bytes=64)
+            nc.sync.dma_start(out=rows[g, t][:], in_=x_rows[g, t])
 
-        def load_res(m):
-            nc.sync.dma_start(out=res_rows[m][:], in_=res[m * P : (m + 1) * P, :])
+        def load_scale_row(i, r):
+            by_row = (w1_scales, w2_scales)[i].rearrange("g (q r) n -> r q g n", r=4)
+            nc.sync.dma_start(out=w_planes[i][r:P:32, :, :].bitcast(I32), in_=by_row[r].bitcast(I32))
 
-        load_res(0)
-        w_codes = {}
-        for g in range(PASSES):
+        def load_w(g):
             for i, words in enumerate((w1_words, w2_words)):
                 w_codes[i, g] = keep.tile([P, N], U32, name=f"w_codes{i}{g}", align_bytes=64)
                 nc.sync.dma_start(
@@ -67,6 +59,22 @@ def tile_picked_highway_gelu_l_kernel(
                     in_=words[g].rearrange("p n t -> p (n t)").bitcast(I32),
                 )
 
+        def load_res(m):
+            res_rows[m] = keep.tile([P, T], F32, name=f"res{m}")
+            nc.sync.dma_start(out=res_rows[m][:], in_=res[m * P : (m + 1) * P, :])
+
+        load_x(0, 0)
+        nc.sync.dma_start(offsets[:], offs)
+        load_x(0, 1)
+        for r, (g, t) in enumerate(((0, 2), (0, 3), (1, 0), (1, 1))):
+            load_x(g, t)
+            load_scale_row(0, r)
+            load_scale_row(1, r)
+        load_x(1, 2)
+        load_w(0)
+        load_x(1, PACK - 1)
+        load_res(0)
+        load_w(1)
         load_res(1)
 
         zero_in = keep.tile([P, 1], F32, name="zero_in")
@@ -74,74 +82,63 @@ def tile_picked_highway_gelu_l_kernel(
         nc.vector.memset(zero_in[:], 0.0)
         nc.scalar.activation(out=zero_bias[:], in_=zero_in[:], func=ACT.Gelu_apprx_tanh)
 
-        vector_cols = {(0, 0, 0): 0, (0, 0, 512): 352, (0, 1, 0): 704, (1, 0, 0): 1024, (1, 1, 0): 0, (1, 1, 512): 288}
-        x_codes, x_planes, pairs, picked = {}, {}, {}, {}
+        picked = [keep.tile([P, PACK, S], BF16, name=f"picked{g}", align_bytes=64) for g in range(PASSES)]
+        woven, x_codes, x_planes = {}, {}, {}
 
-        def cast(g, u):
-            pairs[g, u] = keep.tile([P, T], U32, name=f"pairs{g}{u}")
-            pairs_bf = pairs[g, u][:].bitcast(BF16).rearrange("p (c e) -> p c e", e=2)
-            for c0, c1 in pieces[g, u]:
-                source = raw[g, u, c0][:].rearrange("p e c -> p c e")
-                cut = vector_cols[g, u, c0]
-                if cut < c1 - c0:
-                    nc.scalar.copy(out=pairs_bf[:, c0 + cut : c1, :], in_=source[:, cut:, :])
-                if cut:
-                    nc.vector.tensor_copy(out=pairs_bf[:, c0 : c0 + cut, :], in_=source[:, :cut, :])
+        def gather_scalar(out_ap, window, offsets_ap):
+            nc.scalar.activation(out=out_ap, in_=window[:].indirect(offsets_ap), func=ACT.Copy)
 
-        def gather(g, u, halves=(0, 1)):
-            for h in halves:
-                if u == 0:
-                    tag = "raw11_0" if (g, h) == (1, 1) else f"picked{g}{h}"
-                    picked[g, h] = keep.tile([P, 2, HALF], U32, name=f"picked{g}{h}", tag=tag, align_bytes=64)
-                nc.vector.tensor_copy(picked[g, h][:, u, :], pairs[g, u][:].indirect(half_offsets[h]))
+        def gather_vector(out_ap, window, offsets_ap):
+            nc.vector.tensor_copy(out_ap, window[:].indirect(offsets_ap))
 
-        woven = {}
+        def weave(g, h, copy):
+            woven[g, h] = keep.tile([P, HALF * PACK], BF16, name=f"woven{g}{h}", align_bytes=64)
+            copy(
+                out=woven[g, h][:].rearrange("p (c i t) -> p c t i", i=4, t=PACK),
+                in_=picked[g][:, :, halves[h]].rearrange("p t (c i) -> p c t i", i=4),
+            )
 
-        def weave(g):
-            for h in range(2):
-                woven[g, h] = keep.tile([P, 2 * HALF], U32, name=f"woven{g}{h}", tag=f"woven{g}{h}", align_bytes=64)
-                nc.scalar.copy(
-                    out=woven[g, h][:].rearrange("p (j u) -> p j u", u=2),
-                    in_=picked[g, h][:].rearrange("p u j -> p j u"),
-                )
+        def quantise(g, h):
+            x_codes[g, h] = keep.tile([P, HALF], U32, name=f"x_codes{g}{h}", align_bytes=64)
+            x_planes[g, h] = keep.tile([P, HALF], U8, name=f"x_planes{g}{h}", align_bytes=64)
+            nc.vector.quantize_mx(out=x_codes[g, h][:].bitcast(FP8X4), scales=x_planes[g, h][:], in_=woven[g, h][:])
 
-        def quantise(g, tag):
-            codes = keep.tile([P, S], U32, name=f"x_codes{g}", tag=tag, align_bytes=64)
-            for h in range(2):
-                x_codes[g, h] = codes[:, h * HALF : (h + 1) * HALF]
-                x_planes[g, h] = keep.tile([P, HALF], U8, name=f"x_planes{g}{h}", align_bytes=64)
-                nc.vector.quantize_mx(
-                    out=x_codes[g, h].bitcast(FP8X4),
-                    scales=x_planes[g, h][:],
-                    in_=woven[g, h][:].bitcast(BF16),
-                )
+        def gather_shared(g, t):
+            gather_vector(picked[g][:, t, halves[0]], rows[g, t], half_offsets[0])
+            gather_scalar(picked[g][:, t, halves[1]], rows[g, t], half_offsets[1])
 
-        cast(0, 0)
-        gather(0, 0)
-        cast(0, 1)
-        gather(0, 1)
-        weave(0)
-        cast(1, 0)
-        quantise(0, "raw10_0")
-        gather(1, 0, (0,))
-        cast(1, 1)
-        gather(1, 0, (1,))
-        gather(1, 1)
-        weave(1)
-        quantise(1, "x_codes1")
-
-        passing = [
-            keep.tile([P, HALF], F32, name="passing0"),
-            keep.tile([P, HALF], F32, name="passing1", tag="woven11", align_bytes=64),
-        ]
+        gather_scalar(picked[0][:, 0, :], rows[0, 0], offsets[:])
+        gather_vector(picked[0][:, 1, :], rows[0, 1], offsets[:])
+        gather_scalar(picked[0][:, 2, :], rows[0, 2], offsets[:])
+        gather_shared(0, 3)
         for h in range(2):
-            nc.vector.tensor_copy(passing[h][:], res_rows[0][:].indirect(half_offsets[h]))
+            weave(0, h, nc.vector.tensor_copy)
+        for h in range(2):
+            quantise(0, h)
+
+        last = PACK - 1
+        gather_scalar(picked[1][:, 0, :], rows[1, 0], offsets[:])
+        gather_shared(1, 1)
+        gather_shared(1, 2)
+        slots = {}
+        for h in range(2):
+            woven[1, h] = keep.tile([P, HALF * PACK], BF16, name=f"woven1{h}", tag=f"woven1{h}", align_bytes=64)
+            slots[h] = woven[1, h][:].rearrange("p (c t) -> p c t", t=PACK)
+            nc.vector.tensor_copy(
+                out=slots[h][:, :, 0:last],
+                in_=picked[1][:, 0:last, halves[h]].rearrange("p t c -> p c t"),
+            )
+        gather_vector(slots[0][:, :, last], rows[1, last], half_offsets[0])
+        gather_scalar(picked[1][:, last, halves[1]], rows[1, last], half_offsets[1])
+        nc.vector.tensor_copy(out=slots[1][:, :, last], in_=picked[1][:, last, halves[1]])
+        quantise(1, 0)
+        quantise(1, 1)
 
         sums = {}
         for g in range(PASSES):
-            for i in range(2):
+            for m in range(M_TILES):
                 for h in range(2):
-                    for m in range(M_TILES):
+                    for i in range(2):
                         if g == 0:
                             sums[h, i, m] = psum.tile([P, HALF], F32, name=f"sum{h}{i}{m}")
                         cols = slice(m * P, (m + 1) * P)
@@ -149,39 +146,51 @@ def tile_picked_highway_gelu_l_kernel(
                             out=sums[h, i, m][:],
                             lhsT=w_codes[i, g][:, cols].bitcast(FP8X4),
                             lhsT_scale=w_planes[i][:, g, cols],
-                            rhs=x_codes[g, h].bitcast(FP8X4),
+                            rhs=x_codes[g, h][:].bitcast(FP8X4),
                             rhs_scale=x_planes[g, h][:],
                             start=(g == 0),
                             stop=(g == PASSES - 1),
                         )
-        y = [keep.tile([P, S], F32, name=f"y{m}") for m in range(M_TILES)]
-        th = [keep.tile([P, S], F32, name=f"th{m}") for m in range(M_TILES)]
-        d = [keep.tile([P, S], F32, name=f"d{m}") for m in range(M_TILES)]
-        e = [keep.tile([P, S], F32, name=f"e{m}") for m in range(M_TILES)]
-        o = [keep.tile([P, S], F32, name=f"o{m}") for m in range(M_TILES)]
-        for h in range(2):
-            cols = slice(h * HALF, (h + 1) * HALF)
-            for m in range(M_TILES):
-                nc.scalar.activation(out=y[m][:, cols], in_=sums[h, 0, m][:], func=ACT.Gelu_apprx_tanh, bias=zero_bias[:])
-        for m in range(M_TILES):
-            for h in range(2):
-                cols = slice(h * HALF, (h + 1) * HALF)
-                nc.scalar.activation(out=th[m][:, cols], in_=sums[h, 1, m][:], func=ACT.Tanh, bias=zero_bias[:], scale=0.5)
-        for h in range(2):
-            cols = slice(h * HALF, (h + 1) * HALF)
-            nc.vector.tensor_tensor(d[0][:, cols], passing[h][:], y[0][:, cols], ALU.subtract)
-        nc.vector.tensor_tensor(d[1][:], res_rows[1][:].indirect(offsets[:]), y[1][:], ALU.subtract)
 
-        def gate(m, cols):
-            nc.vector.scalar_tensor_tensor(e[m][:, cols], th[m][:, cols], 1.0, d[m][:, cols], ALU.subtract, ALU.mult)
+        passing, y, th, diff, gated = {}, {}, {}, {}, {}
+        blocks = [(m, h) for m in range(M_TILES) for h in range(2)]
 
-        def finish(m, cols):
-            nc.vector.scalar_tensor_tensor(o[m][:, cols], e[m][:, cols], -0.5, y[m][:, cols], ALU.mult, ALU.add)
-            nc.sync.dma_start(out=out[m * P : (m + 1) * P, cols], in_=o[m][:, cols])
+        def fetch(b, gather):
+            m, h = blocks[b]
+            passing[b] = keep.tile([P, HALF], F32, name=f"passing{b}", tag=("woven11", "rows13")[h], align_bytes=64)
+            gather(passing[b][:], res_rows[m], half_offsets[h])
 
-        gate(0, slice(0, S))
-        gate(1, slice(0, HALF))
-        finish(0, slice(0, S))
-        gate(1, slice(HALF, S))
-        finish(1, slice(0, HALF))
-        finish(1, slice(HALF, S))
+        def activate(b):
+            m, h = blocks[b]
+            y[b] = keep.tile([P, HALF], F32, name=f"y{b}")
+            th[b] = keep.tile([P, HALF], F32, name=f"th{b}")
+            nc.scalar.activation(out=y[b][:], in_=sums[h, 0, m][:], func=ACT.Gelu_apprx_tanh, bias=zero_bias[:])
+            nc.scalar.activation(out=th[b][:], in_=sums[h, 1, m][:], func=ACT.Tanh, bias=zero_bias[:], scale=0.5)
+
+        def subtract(b):
+            diff[b] = keep.tile([P, HALF], F32, name=f"diff{b}")
+            nc.vector.tensor_tensor(diff[b][:], passing[b][:], y[b][:], ALU.subtract)
+
+        def gate(b):
+            gated[b] = keep.tile([P, HALF], F32, name=f"gated{b}")
+            nc.vector.scalar_tensor_tensor(gated[b][:], th[b][:], 1.0, diff[b][:], ALU.subtract, ALU.mult)
+
+        def finish(b):
+            m, h = blocks[b]
+            result = keep.tile([P, HALF], F32, name=f"result{b}")
+            nc.vector.scalar_tensor_tensor(result[:], gated[b][:], -0.5, y[b][:], ALU.mult, ALU.add)
+            nc.sync.dma_start(out=out[m * P : (m + 1) * P, halves[h]], in_=result[:])
+
+        fetch(0, gather_vector)
+        fetch(1, gather_scalar)
+        activate(0)
+        activate(1)
+        subtract(0)
+        for b in range(len(blocks)):
+            gate(b)
+            if b + 1 < len(blocks):
+                subtract(b + 1)
+            if b + 2 < len(blocks):
+                fetch(b + 2, gather_scalar)
+                activate(b + 2)
+            finish(b)

@@ -20,6 +20,7 @@ PACK = 4
 PASSES = K // (P * PACK)
 HALF = S // 2
 M_TILES = N // P
+VECTOR_SHARE = 320
 
 
 def tile_picked_highway_gelu_l_kernel(
@@ -38,7 +39,7 @@ def tile_picked_highway_gelu_l_kernel(
         w_planes = []
         for i in range(2):
             plane = keep.tile([P, PASSES, N], U8, name=f"w_planes{i}", align_bytes=64)
-            nc.vector.memset(plane[:].bitcast(I32), 0)
+            nc.gpsimd.memset(plane[:].bitcast(I32), 0)
             w_planes.append(plane)
 
         rows, w_codes, res_rows = {}, {}, {}
@@ -51,38 +52,42 @@ def tile_picked_highway_gelu_l_kernel(
             by_row = (w1_scales, w2_scales)[i].rearrange("g (q r) n -> r q g n", r=4)
             nc.sync.dma_start(out=w_planes[i][r:P:32, :, :].bitcast(I32), in_=by_row[r].bitcast(I32))
 
-        def load_w(g):
+        def load_w(g, blocks):
+            cols = slice(blocks[0] * P, (blocks[-1] + 1) * P)
             for i, words in enumerate((w1_words, w2_words)):
-                w_codes[i, g] = keep.tile([P, N], U32, name=f"w_codes{i}{g}", align_bytes=64)
+                codes = keep.tile([P, len(blocks), P], U32, name=f"w_codes{i}{g}{blocks[0]}", align_bytes=64)
                 nc.sync.dma_start(
-                    out=w_codes[i, g][:].bitcast(I32),
-                    in_=words[g].rearrange("p n t -> p (n t)").bitcast(I32),
+                    out=codes[:].rearrange("p m n -> p (m n)").bitcast(I32),
+                    in_=words[g].rearrange("p n t -> p (n t)").bitcast(I32)[:, cols],
                 )
+                for m in blocks:
+                    w_codes[i, g, m] = codes[:, m - blocks[0], :]
 
         def load_res(m):
-            res_rows[m] = keep.tile([P, T], F32, name=f"res{m}")
+            res_rows[m] = keep.tile([P, T], F32, name=f"res{m}", tag=f"res{m}")
             nc.sync.dma_start(out=res_rows[m][:], in_=res[m * P : (m + 1) * P, :])
 
         load_x(0, 0)
         nc.sync.dma_start(offsets[:], offs)
-        load_x(0, 1)
-        for r, (g, t) in enumerate(((0, 2), (0, 3), (1, 0), (1, 1))):
+        scale_rows = [(i, r) for i in range(2) for r in range(4)]
+        for n, (g, t) in enumerate(((0, 1), (0, 2), (0, 3), (1, 0), (1, 1), (1, 2))):
             load_x(g, t)
-            load_scale_row(0, r)
-            load_scale_row(1, r)
-        load_x(1, 2)
-        load_w(0)
+            load_scale_row(*scale_rows[n])
+        load_w(0, (0, 1))
         load_x(1, PACK - 1)
+        for i, r in scale_rows[6:]:
+            load_scale_row(i, r)
         load_res(0)
-        load_w(1)
+        load_w(1, (0,))
         load_res(1)
+        load_w(1, (1,))
 
         zero_in = keep.tile([P, 1], F32, name="zero_in")
         zero_bias = keep.tile([P, 1], F32, name="zero_bias")
         nc.vector.memset(zero_in[:], 0.0)
         nc.scalar.activation(out=zero_bias[:], in_=zero_in[:], func=ACT.Gelu_apprx_tanh)
 
-        picked = [keep.tile([P, PACK, S], BF16, name=f"picked{g}", align_bytes=64) for g in range(PASSES)]
+        picked = [keep.tile([P, PACK, S], BF16, name=f"picked{g}", tag=f"picked{g}", align_bytes=64) for g in range(PASSES)]
         woven, x_codes, x_planes = {}, {}, {}
 
         def gather_scalar(out_ap, window, offsets_ap):
@@ -101,7 +106,7 @@ def tile_picked_highway_gelu_l_kernel(
         def quantise(g, h):
             x_codes[g, h] = keep.tile([P, HALF], U32, name=f"x_codes{g}{h}", align_bytes=64)
             x_planes[g, h] = keep.tile([P, HALF], U8, name=f"x_planes{g}{h}", align_bytes=64)
-            nc.vector.quantize_mx(out=x_codes[g, h][:].bitcast(FP8X4), scales=x_planes[g, h][:], in_=woven[g, h][:])
+            nc.vector.quantize_mx(out=x_codes[g, h][:].bitcast(FP8X4), scales=x_planes[g, h][:], in_=woven[g, h][:, :])
 
         def gather_shared(g, t):
             gather_vector(picked[g][:, t, halves[0]], rows[g, t], half_offsets[0])
@@ -120,31 +125,31 @@ def tile_picked_highway_gelu_l_kernel(
         gather_scalar(picked[1][:, 0, :], rows[1, 0], offsets[:])
         gather_shared(1, 1)
         gather_shared(1, 2)
-        slots = {}
+        woven_last = keep.tile([P, S * PACK], BF16, name="woven_last", align_bytes=64)
+        slots = woven_last[:].rearrange("p (c t) -> p c t", t=PACK)
         for h in range(2):
-            woven[1, h] = keep.tile([P, HALF * PACK], BF16, name=f"woven1{h}", tag=f"woven1{h}", align_bytes=64)
-            slots[h] = woven[1, h][:].rearrange("p (c t) -> p c t", t=PACK)
+            woven[1, h] = woven_last[:, h * HALF * PACK : (h + 1) * HALF * PACK]
             nc.vector.tensor_copy(
-                out=slots[h][:, :, 0:last],
+                out=slots[:, halves[h], 0:last],
                 in_=picked[1][:, 0:last, halves[h]].rearrange("p t c -> p c t"),
             )
-        gather_vector(slots[0][:, :, last], rows[1, last], half_offsets[0])
-        gather_scalar(picked[1][:, last, halves[1]], rows[1, last], half_offsets[1])
-        nc.vector.tensor_copy(out=slots[1][:, :, last], in_=picked[1][:, last, halves[1]])
+        gather_vector(slots[:, :VECTOR_SHARE, last], rows[1, last], offsets[:, : VECTOR_SHARE // 16])
+        gather_scalar(picked[1][:, last, VECTOR_SHARE:], rows[1, last], offsets[:, VECTOR_SHARE // 16 :])
+        nc.vector.tensor_copy(out=slots[:, VECTOR_SHARE:, last], in_=picked[1][:, last, VECTOR_SHARE:])
         quantise(1, 0)
         quantise(1, 1)
 
         sums = {}
         for g in range(PASSES):
             for m in range(M_TILES):
-                for h in range(2):
-                    for i in range(2):
+                for i in range(2):
+                    for h in range(2):
                         if g == 0:
                             sums[h, i, m] = psum.tile([P, HALF], F32, name=f"sum{h}{i}{m}")
                         cols = slice(m * P, (m + 1) * P)
                         nc.tensor.matmul_mx(
                             out=sums[h, i, m][:],
-                            lhsT=w_codes[i, g][:, cols].bitcast(FP8X4),
+                            lhsT=w_codes[i, g, m].bitcast(FP8X4),
                             lhsT_scale=w_planes[i][:, g, cols],
                             rhs=x_codes[g, h][:].bitcast(FP8X4),
                             rhs_scale=x_planes[g, h][:],
@@ -152,45 +157,49 @@ def tile_picked_highway_gelu_l_kernel(
                             stop=(g == PASSES - 1),
                         )
 
-        passing, y, th, diff, gated = {}, {}, {}, {}, {}
+        passing, y, th, diff, gated, acts = {}, {}, {}, {}, {}, {}
         blocks = [(m, h) for m in range(M_TILES) for h in range(2)]
 
         def fetch(b, gather):
             m, h = blocks[b]
-            passing[b] = keep.tile([P, HALF], F32, name=f"passing{b}", tag=("woven11", "rows13")[h], align_bytes=64)
+            passing[b] = keep.tile([P, HALF], F32, name=f"passing{b}", tag=("rows13", "picked1", "passing2")[b], align_bytes=64)
             gather(passing[b][:], res_rows[m], half_offsets[h])
 
-        def activate(b):
+        def activate(b, func):
             m, h = blocks[b]
-            y[b] = keep.tile([P, HALF], F32, name=f"y{b}")
-            th[b] = keep.tile([P, HALF], F32, name=f"th{b}")
-            nc.scalar.activation(out=y[b][:], in_=sums[h, 0, m][:], func=ACT.Gelu_apprx_tanh, bias=zero_bias[:])
-            nc.scalar.activation(out=th[b][:], in_=sums[h, 1, m][:], func=ACT.Tanh, bias=zero_bias[:], scale=0.5)
+            if func == ACT.Tanh:
+                th[b] = acts[m][:, 2 + h, :]
+                nc.scalar.activation(out=th[b], in_=sums[h, 1, m][:], func=func, bias=zero_bias[:], scale=0.5)
+            else:
+                y[b] = acts[m][:, h, :]
+                nc.scalar.activation(out=y[b], in_=sums[h, 0, m][:], func=func, bias=zero_bias[:])
 
         def subtract(b):
             diff[b] = keep.tile([P, HALF], F32, name=f"diff{b}")
-            nc.vector.tensor_tensor(diff[b][:], passing[b][:], y[b][:], ALU.subtract)
+            m, h = blocks[b]
+            looked_up = passing[b][:] if b in passing else res_rows[m][:].indirect(half_offsets[h])
+            nc.vector.tensor_tensor(diff[b][:], looked_up, y[b], ALU.subtract)
 
         def gate(b):
             gated[b] = keep.tile([P, HALF], F32, name=f"gated{b}")
-            nc.vector.scalar_tensor_tensor(gated[b][:], th[b][:], 1.0, diff[b][:], ALU.subtract, ALU.mult)
+            nc.vector.scalar_tensor_tensor(gated[b][:], th[b], 1.0, diff[b][:], ALU.subtract, ALU.mult)
 
         def finish(b):
             m, h = blocks[b]
             result = keep.tile([P, HALF], F32, name=f"result{b}")
-            nc.vector.scalar_tensor_tensor(result[:], gated[b][:], -0.5, y[b][:], ALU.mult, ALU.add)
+            nc.vector.scalar_tensor_tensor(result[:], gated[b][:], -0.5, y[b], ALU.mult, ALU.add)
             nc.sync.dma_start(out=out[m * P : (m + 1) * P, halves[h]], in_=result[:])
 
-        fetch(0, gather_vector)
-        fetch(1, gather_scalar)
-        activate(0)
-        activate(1)
-        subtract(0)
-        for b in range(len(blocks)):
-            gate(b)
-            if b + 1 < len(blocks):
-                subtract(b + 1)
-            if b + 2 < len(blocks):
-                fetch(b + 2, gather_scalar)
-                activate(b + 2)
-            finish(b)
+        fetch(0, gather_scalar)
+        fetch(1, gather_vector)
+        for m in range(M_TILES):
+            pair = (2 * m, 2 * m + 1)
+            acts[m] = keep.tile([P, 4, HALF], F32, name=f"acts{m}")
+            for func in (ACT.Gelu_apprx_tanh, ACT.Tanh):
+                for b in pair:
+                    activate(b, func)
+            for step in (subtract, gate, finish):
+                for b in pair:
+                    step(b)
+                if m == 0 and step is subtract:
+                    fetch(2, gather_scalar)

@@ -104,7 +104,7 @@ def tile_picked_highway_gelu_l_kernel(
             )
 
         def quantise(g, h):
-            x_codes[g, h] = keep.tile([P, HALF], U32, name=f"x_codes{g}{h}", align_bytes=64)
+            x_codes[g, h] = keep.tile([P, HALF], U32, name=f"x_codes{g}{h}", tag=("rows13" if (g, h) == (1, 0) else f"x_codes{g}{h}"), align_bytes=64)
             x_planes[g, h] = keep.tile([P, HALF], U8, name=f"x_planes{g}{h}", align_bytes=64)
             nc.vector.quantize_mx(out=x_codes[g, h][:].bitcast(FP8X4), scales=x_planes[g, h][:], in_=woven[g, h][:, :])
 
@@ -162,7 +162,7 @@ def tile_picked_highway_gelu_l_kernel(
 
         def fetch(b, gather):
             m, h = blocks[b]
-            passing[b] = keep.tile([P, HALF], F32, name=f"passing{b}", tag=("rows13", "picked1", "passing2")[b], align_bytes=64)
+            passing[b] = keep.tile([P, HALF], F32, name=f"passing{b}", tag=("passing0", "picked1", "passing2")[b], align_bytes=64)
             gather(passing[b][:], res_rows[m], half_offsets[h])
 
         def activate(b, func):

@@ -21,6 +21,7 @@ PASSES = K // (P * PACK)
 HALF = S // 2
 M_TILES = N // P
 VECTOR_SHARE = 320
+SCALAR_WEAVE = 384
 
 
 def tile_picked_highway_gelu_l_kernel(
@@ -52,9 +53,10 @@ def tile_picked_highway_gelu_l_kernel(
             by_row = (w1_scales, w2_scales)[i].rearrange("g (q r) n -> r q g n", r=4)
             nc.sync.dma_start(out=w_planes[i][r:P:32, :, :].bitcast(I32), in_=by_row[r].bitcast(I32))
 
-        def load_w(g, blocks):
+        def load_w(g, blocks, weights=(0, 1)):
             cols = slice(blocks[0] * P, (blocks[-1] + 1) * P)
-            for i, words in enumerate((w1_words, w2_words)):
+            for i in weights:
+                words = (w1_words, w2_words)[i]
                 codes = keep.tile([P, len(blocks), P], U32, name=f"w_codes{i}{g}{blocks[0]}", align_bytes=64)
                 nc.sync.dma_start(
                     out=codes[:].rearrange("p m n -> p (m n)").bitcast(I32),
@@ -70,13 +72,16 @@ def tile_picked_highway_gelu_l_kernel(
         load_x(0, 0)
         nc.sync.dma_start(offsets[:], offs)
         scale_rows = [(i, r) for i in range(2) for r in range(4)]
-        for n, (g, t) in enumerate(((0, 1), (0, 2), (0, 3), (1, 0), (1, 1), (1, 2))):
+        rows_behind = {(0, 1): 1, (0, 2): 1, (0, 3): 1, (1, 0): 1, (1, 1): 1, (1, 2): 1}
+        for (g, t), count in rows_behind.items():
             load_x(g, t)
-            load_scale_row(*scale_rows[n])
-        load_w(0, (0, 1))
+            for n in range(count):
+                load_scale_row(*scale_rows.pop(0))
+        load_w(0, (0, 1), (0,))
         load_x(1, PACK - 1)
-        for i, r in scale_rows[6:]:
+        for i, r in scale_rows:
             load_scale_row(i, r)
+        load_w(0, (0, 1), (1,))
         load_res(0)
         load_w(1, (0,))
         load_res(1)
@@ -108,14 +113,16 @@ def tile_picked_highway_gelu_l_kernel(
             x_planes[g, h] = keep.tile([P, HALF], U8, name=f"x_planes{g}{h}", align_bytes=64)
             nc.vector.quantize_mx(out=x_codes[g, h][:].bitcast(FP8X4), scales=x_planes[g, h][:], in_=woven[g, h][:, :])
 
-        def gather_shared(g, t):
-            gather_vector(picked[g][:, t, halves[0]], rows[g, t], half_offsets[0])
-            gather_scalar(picked[g][:, t, halves[1]], rows[g, t], half_offsets[1])
+        def gather_shared(g, t, vector_cuts):
+            for a, b in zip(vector_cuts, vector_cuts[1:]):
+                gather_vector(picked[g][:, t, a:b], rows[g, t], offsets[:, a // 16 : b // 16])
+            cut = vector_cuts[-1]
+            gather_scalar(picked[g][:, t, cut:], rows[g, t], offsets[:, cut // 16 :])
 
         gather_scalar(picked[0][:, 0, :], rows[0, 0], offsets[:])
         gather_vector(picked[0][:, 1, :], rows[0, 1], offsets[:])
         gather_scalar(picked[0][:, 2, :], rows[0, 2], offsets[:])
-        gather_shared(0, 3)
+        gather_shared(0, 3, (0, HALF))
         for h in range(2):
             weave(0, h, nc.vector.tensor_copy)
         for h in range(2):
@@ -123,16 +130,19 @@ def tile_picked_highway_gelu_l_kernel(
 
         last = PACK - 1
         gather_scalar(picked[1][:, 0, :], rows[1, 0], offsets[:])
-        gather_shared(1, 1)
-        gather_shared(1, 2)
+        gather_shared(1, 1, (0, 128))
+        gather_shared(1, 2, (0, 96, 192))
         woven_last = keep.tile([P, S * PACK], BF16, name="woven_last", align_bytes=64)
         slots = woven_last[:].rearrange("p (c t) -> p c t", t=PACK)
         for h in range(2):
             woven[1, h] = woven_last[:, h * HALF * PACK : (h + 1) * HALF * PACK]
-            nc.vector.tensor_copy(
-                out=slots[:, halves[h], 0:last],
-                in_=picked[1][:, 0:last, halves[h]].rearrange("p t c -> p c t"),
-            )
+        for copy, cols in (
+            (nc.vector.tensor_copy, slice(0, 96)),
+            (nc.vector.tensor_copy, slice(96, 192)),
+            (nc.vector.tensor_copy, slice(192, SCALAR_WEAVE)),
+            (nc.scalar.copy, slice(SCALAR_WEAVE, S)),
+        ):
+            copy(out=slots[:, cols, 0:last], in_=picked[1][:, 0:last, cols].rearrange("p t c -> p c t"))
         gather_vector(slots[:, :VECTOR_SHARE, last], rows[1, last], offsets[:, : VECTOR_SHARE // 16])
         gather_scalar(picked[1][:, last, VECTOR_SHARE:], rows[1, last], offsets[:, VECTOR_SHARE // 16 :])
         nc.vector.tensor_copy(out=slots[:, VECTOR_SHARE:, last], in_=picked[1][:, last, VECTOR_SHARE:])

@@ -20,7 +20,7 @@ PACK = 4
 PASSES = K // (P * PACK)
 HALF = S // 2
 M_TILES = N // P
-VECTOR_SHARE = 320
+VECTOR_SHARE = 256
 SCALAR_WEAVE = 384
 
 
@@ -84,8 +84,9 @@ def tile_picked_highway_gelu_l_kernel(
         load_w(0, (0, 1), (1,))
         load_res(0)
         load_w(1, (0,))
+        load_w(1, (1,), (0,))
         load_res(1)
-        load_w(1, (1,))
+        load_w(1, (1,), (1,))
 
         zero_in = keep.tile([P, 1], F32, name="zero_in")
         zero_bias = keep.tile([P, 1], F32, name="zero_bias")
@@ -172,7 +173,7 @@ def tile_picked_highway_gelu_l_kernel(
 
         def fetch(b, gather):
             m, h = blocks[b]
-            passing[b] = keep.tile([P, HALF], F32, name=f"passing{b}", tag=("passing0", "picked1", "passing2")[b], align_bytes=64)
+            passing[b] = keep.tile([P, HALF], F32, name=f"passing{b}", tag=("picked1" if b == 1 else f"passing{b}"), align_bytes=64)
             gather(passing[b][:], res_rows[m], half_offsets[h])
 
         def activate(b, func):
@@ -196,9 +197,13 @@ def tile_picked_highway_gelu_l_kernel(
 
         def finish(b):
             m, h = blocks[b]
-            result = keep.tile([P, HALF], F32, name=f"result{b}")
-            nc.vector.scalar_tensor_tensor(result[:], gated[b][:], -0.5, y[b], ALU.mult, ALU.add)
-            nc.sync.dma_start(out=out[m * P : (m + 1) * P, halves[h]], in_=result[:])
+            pieces = 2 if b == len(blocks) - 1 else 1
+            width = HALF // pieces
+            for n in range(pieces):
+                cols = slice(n * width, (n + 1) * width)
+                result = keep.tile([P, width], F32, name=f"result{b}{n}")
+                nc.vector.scalar_tensor_tensor(result[:], gated[b][:, cols], -0.5, y[b][:, cols], ALU.mult, ALU.add)
+                nc.sync.dma_start(out=out[m * P : (m + 1) * P, halves[h]][:, cols], in_=result[:])
 
         fetch(0, gather_scalar)
         fetch(1, gather_vector)
@@ -207,9 +212,9 @@ def tile_picked_highway_gelu_l_kernel(
             acts[m] = keep.tile([P, 4, HALF], F32, name=f"acts{m}")
             for func in (ACT.Gelu_apprx_tanh, ACT.Tanh):
                 for b in pair:
+                    if b == 3 and func != ACT.Tanh:
+                        fetch(b, gather_scalar)
                     activate(b, func)
             for step in (subtract, gate, finish):
                 for b in pair:
                     step(b)
-                if m == 0 and step is subtract:
-                    fetch(2, gather_scalar)

@@ -51,19 +51,18 @@ def tile_picked_highway_gelu_l_kernel(
 
         def load_scale_row(i, r):
             by_row = (w1_scales, w2_scales)[i].rearrange("g (q r) n -> r q g n", r=4)
-            nc.sync.dma_start(out=w_planes[i][r:P:32, :, :].bitcast(I32), in_=by_row[r].bitcast(I32))
+            nc.sync.dma_start(out=w_planes[i][8 * i + r : P : 32, :, :].bitcast(I32), in_=by_row[r].bitcast(I32))
 
-        def load_w(g, blocks, weights=(0, 1)):
-            cols = slice(blocks[0] * P, (blocks[-1] + 1) * P)
-            for i in weights:
-                words = (w1_words, w2_words)[i]
-                codes = keep.tile([P, len(blocks), P], U32, name=f"w_codes{i}{g}{blocks[0]}", align_bytes=64)
-                nc.sync.dma_start(
-                    out=codes[:].rearrange("p m n -> p (m n)").bitcast(I32),
-                    in_=words[g].rearrange("p n t -> p (n t)").bitcast(I32)[:, cols],
-                )
+        def load_w(i, passes, blocks):
+            codes = keep.tile([P, len(passes), len(blocks) * P], U32, name=f"w_codes{i}{passes[0]}{blocks[0]}", align_bytes=64)
+            by_pass = (w1_words, w2_words)[i].rearrange("g p n t -> p g (n t)").bitcast(I32)
+            nc.sync.dma_start(
+                out=codes[:].bitcast(I32),
+                in_=by_pass[:, passes[0] : passes[-1] + 1, blocks[0] * P : (blocks[-1] + 1) * P],
+            )
+            for g in passes:
                 for m in blocks:
-                    w_codes[i, g, m] = codes[:, m - blocks[0], :]
+                    w_codes[i, g, m] = codes[:, g - passes[0], (m - blocks[0]) * P : (m - blocks[0] + 1) * P]
 
         def load_res(m):
             res_rows[m] = keep.tile([P, T], F32, name=f"res{m}", tag=f"res{m}")
@@ -77,14 +76,16 @@ def tile_picked_highway_gelu_l_kernel(
             load_x(g, t)
             for n in range(count):
                 load_scale_row(*scale_rows.pop(0))
-        load_w(0, (0, 1), (0,))
+        load_w(0, (0,), (0, 1))
         load_x(1, PACK - 1)
         for i, r in scale_rows:
             load_scale_row(i, r)
-        load_w(0, (0, 1), (1,))
+        load_w(1, (0,), (0,))
         load_res(0)
-        load_w(1, (0,))
+        load_w(0, (1,), (0,))
         load_w(1, (1,), (0,))
+        load_w(0, (1,), (1,))
+        load_w(1, (0,), (1,))
         load_res(1)
         load_w(1, (1,), (1,))
 
@@ -151,17 +152,17 @@ def tile_picked_highway_gelu_l_kernel(
         quantise(1, 1)
 
         sums = {}
-        for g in range(PASSES):
-            for m in range(M_TILES):
-                for i in range(2):
-                    for h in range(2):
+        for m in range(M_TILES):
+            for i in range(2):
+                for h in range(2):
+                    for g in range(PASSES):
                         if g == 0:
                             sums[h, i, m] = psum.tile([P, HALF], F32, name=f"sum{h}{i}{m}")
                         cols = slice(m * P, (m + 1) * P)
                         nc.tensor.matmul_mx(
                             out=sums[h, i, m][:],
                             lhsT=w_codes[i, g, m].bitcast(FP8X4),
-                            lhsT_scale=w_planes[i][:, g, cols],
+                            lhsT_scale=w_planes[i][8 * i : P, g, cols],
                             rhs=x_codes[g, h][:].bitcast(FP8X4),
                             rhs_scale=x_planes[g, h][:],
                             start=(g == 0),

@@ -51,7 +51,7 @@ def tile_picked_highway_gelu_l_kernel(
 
         def load_scale_row(i, r):
             by_row = (w1_scales, w2_scales)[i].rearrange("g (q r) n -> r q g n", r=4)
-            nc.sync.dma_start(out=w_planes[i][8 * i + r : P : 32, :, :].bitcast(I32), in_=by_row[r].bitcast(I32))
+            (nc.scalar, nc.sync)[i].dma_start(out=w_planes[i][8 * i + r : P : 32, :, :].bitcast(I32), in_=by_row[r].bitcast(I32))
 
         def load_w(i, passes, blocks):
             codes = keep.tile([P, len(passes), len(blocks) * P], U32, name=f"w_codes{i}{passes[0]}{blocks[0]}", align_bytes=64)
@@ -71,14 +71,13 @@ def tile_picked_highway_gelu_l_kernel(
         load_x(0, 0)
         nc.sync.dma_start(offsets[:], offs)
         scale_rows = [(i, r) for i in range(2) for r in range(4)]
-        rows_behind = {(0, 1): 1, (0, 2): 1, (0, 3): 1, (1, 0): 1, (1, 1): 1, (1, 2): 1}
-        for (g, t), count in rows_behind.items():
+        for i, r in scale_rows[:4]:
+            load_scale_row(i, r)
+        for g, t in ((0, 1), (0, 2), (0, 3), (1, 0), (1, 1), (1, 2)):
             load_x(g, t)
-            for n in range(count):
-                load_scale_row(*scale_rows.pop(0))
         load_w(0, (0,), (0, 1))
         load_x(1, PACK - 1)
-        for i, r in scale_rows:
+        for i, r in scale_rows[4:]:
             load_scale_row(i, r)
         load_w(1, (0,), (0,))
         load_res(0)
@@ -91,7 +90,7 @@ def tile_picked_highway_gelu_l_kernel(
 
         zero_in = keep.tile([P, 1], F32, name="zero_in")
         zero_bias = keep.tile([P, 1], F32, name="zero_bias")
-        nc.vector.memset(zero_in[:], 0.0)
+        nc.gpsimd.memset(zero_in[:], 0.0)
         nc.scalar.activation(out=zero_bias[:], in_=zero_in[:], func=ACT.Gelu_apprx_tanh)
 
         picked = [keep.tile([P, PACK, S], BF16, name=f"picked{g}", tag=f"picked{g}", align_bytes=64) for g in range(PASSES)]
@@ -192,30 +191,42 @@ def tile_picked_highway_gelu_l_kernel(
             looked_up = passing[b][:] if b in passing else res_rows[m][:].indirect(half_offsets[h])
             nc.vector.tensor_tensor(diff[b][:], looked_up, y[b], ALU.subtract)
 
-        def gate(b):
-            gated[b] = keep.tile([P, HALF], F32, name=f"gated{b}")
-            nc.vector.scalar_tensor_tensor(gated[b][:], th[b], 1.0, diff[b][:], ALU.subtract, ALU.mult)
+        def gate(b, cols=slice(0, HALF)):
+            if b not in gated:
+                gated[b] = keep.tile([P, HALF], F32, name=f"gated{b}")
+            nc.vector.scalar_tensor_tensor(gated[b][:, cols], th[b][:, cols], 1.0, diff[b][:, cols], ALU.subtract, ALU.mult)
 
-        def finish(b):
+        def finish(b, cols=slice(0, HALF)):
             m, h = blocks[b]
-            pieces = 2 if b == len(blocks) - 1 else 1
-            width = HALF // pieces
-            for n in range(pieces):
-                cols = slice(n * width, (n + 1) * width)
-                result = keep.tile([P, width], F32, name=f"result{b}{n}")
-                nc.vector.scalar_tensor_tensor(result[:], gated[b][:, cols], -0.5, y[b][:, cols], ALU.mult, ALU.add)
-                nc.sync.dma_start(out=out[m * P : (m + 1) * P, halves[h]][:, cols], in_=result[:])
+            result = keep.tile([P, cols.stop - cols.start], F32, name=f"result{b}{cols.start}")
+            nc.vector.scalar_tensor_tensor(result[:], gated[b][:, cols], -0.5, y[b][:, cols], ALU.mult, ALU.add)
+            nc.sync.dma_start(out=out[m * P : (m + 1) * P, halves[h]][:, cols], in_=result[:])
 
+        GELU, TANH = ACT.Gelu_apprx_tanh, ACT.Tanh
+        for m in range(M_TILES):
+            acts[m] = keep.tile([P, 4, HALF], F32, name=f"acts{m}")
         fetch(0, gather_scalar)
         fetch(1, gather_vector)
-        for m in range(M_TILES):
-            pair = (2 * m, 2 * m + 1)
-            acts[m] = keep.tile([P, 4, HALF], F32, name=f"acts{m}")
-            for func in (ACT.Gelu_apprx_tanh, ACT.Tanh):
-                for b in pair:
-                    if b == 3 and func != ACT.Tanh:
-                        fetch(b, gather_scalar)
-                    activate(b, func)
-            for step in (subtract, gate, finish):
-                for b in pair:
-                    step(b)
+        for func in (GELU, TANH):
+            for b in (0, 1):
+                activate(b, func)
+        activate(2, GELU)
+        activate(2, TANH)
+        fetch(3, gather_scalar)
+        activate(3, GELU)
+        activate(3, TANH)
+        pieces = (slice(0, HALF // 2), slice(HALF // 2, HALF))
+        subtract(0)
+        subtract(1)
+        gate(0)
+        gate(1)
+        finish(0)
+        subtract(2)
+        finish(1)
+        gate(2)
+        subtract(3)
+        finish(2)
+        for cols in pieces:
+            gate(3, cols)
+        for cols in pieces:
+            finish(3, cols)

@@ -151,15 +151,31 @@ def tile_picked_highway_gelu_l_kernel(
         quantise(1, 1)
 
         sums = {}
+        last_bank = psum.tile([P, S], F32, name="last_bank")
+
+        def warm_up():
+            for width in (HALF, HALF // 2):
+                nc.tensor.matmul_mx(
+                    out=last_bank[:, HALF : HALF + width],
+                    lhsT=w_codes[1, 0, 0].bitcast(FP8X4),
+                    lhsT_scale=w_planes[1][8:P, 0, :P],
+                    rhs=x_codes[0, 1][:, :width].bitcast(FP8X4),
+                    rhs_scale=x_planes[0, 1][:, :width],
+                    start=True,
+                    stop=True,
+                )
+
         for m in range(M_TILES):
             for i in range(2):
                 for h in range(2):
                     for g in range(PASSES):
                         if g == 0:
-                            sums[h, i, m] = psum.tile([P, HALF], F32, name=f"sum{h}{i}{m}")
+                            sums[h, i, m] = (
+                                last_bank[:, :HALF] if (h, i, m) == (1, 1, 1) else psum.tile([P, HALF], F32, name=f"sum{h}{i}{m}")[:]
+                            )
                         cols = slice(m * P, (m + 1) * P)
                         nc.tensor.matmul_mx(
-                            out=sums[h, i, m][:],
+                            out=sums[h, i, m],
                             lhsT=w_codes[i, g, m].bitcast(FP8X4),
                             lhsT_scale=w_planes[i][8 * i : P, g, cols],
                             rhs=x_codes[g, h][:].bitcast(FP8X4),
@@ -167,6 +183,8 @@ def tile_picked_highway_gelu_l_kernel(
                             start=(g == 0),
                             stop=(g == PASSES - 1),
                         )
+            if m == 0:
+                warm_up()
 
         passing, y, th, diff, gated, acts = {}, {}, {}, {}, {}, {}
         blocks = [(m, h) for m in range(M_TILES) for h in range(2)]
@@ -180,10 +198,10 @@ def tile_picked_highway_gelu_l_kernel(
             m, h = blocks[b]
             if func == ACT.Tanh:
                 th[b] = acts[m][:, 2 + h, :]
-                nc.scalar.activation(out=th[b], in_=sums[h, 1, m][:], func=func, bias=zero_bias[:], scale=0.5)
+                nc.scalar.activation(out=th[b], in_=sums[h, 1, m], func=func, bias=zero_bias[:], scale=0.5)
             else:
                 y[b] = acts[m][:, h, :]
-                nc.scalar.activation(out=y[b], in_=sums[h, 0, m][:], func=func, bias=zero_bias[:])
+                nc.scalar.activation(out=y[b], in_=sums[h, 0, m], func=func, bias=zero_bias[:])
 
         def subtract(b):
             diff[b] = keep.tile([P, HALF], F32, name=f"diff{b}")

@@ -19,9 +19,8 @@ P = 128
 PACK = 4
 PASSES = K // (P * PACK)
 HALF = S // 2
+QUARTER = S // 4
 M_TILES = N // P
-VECTOR_SHARE = 256
-SCALAR_WEAVE = 384
 
 
 def tile_picked_highway_gelu_l_kernel(
@@ -34,24 +33,30 @@ def tile_picked_highway_gelu_l_kernel(
 
         offsets = keep.tile([P, S // 16], U16, name="offsets")
         halves = [slice(h * HALF, (h + 1) * HALF) for h in range(2)]
-        half_offsets = [offsets[:, h * (HALF // 16) : (h + 1) * (HALF // 16)] for h in range(2)]
 
-        x_rows = xT.rearrange("(g p t) c -> g t p c", g=PASSES, p=P, t=PACK)
+        def entries(a, b):
+            return offsets[:, a // 16 : b // 16]
+
+        x_rows = xT.rearrange("(g p t) c -> g p (t c)", g=PASSES, p=P, t=PACK)
         w_planes = []
         for i in range(2):
             plane = keep.tile([P, PASSES, N], U8, name=f"w_planes{i}", align_bytes=64)
             nc.gpsimd.memset(plane[:].bitcast(I32), 0)
             w_planes.append(plane)
 
-        rows, w_codes, res_rows = {}, {}, {}
+        windows, w_codes, res_rows = {}, {}, {}
 
-        def load_x(g, t):
-            rows[g, t] = keep.tile([P, T], F32, name=f"rows{g}{t}", tag=f"rows{g}{t}", align_bytes=64)
-            nc.sync.dma_start(out=rows[g, t][:], in_=x_rows[g, t])
+        def load_x(g, t, count):
+            rows = keep.tile([P, count * T], F32, name=f"rows{g}{t}", tag=f"rows{g}{t}", align_bytes=64)
+            nc.sync.dma_start(out=rows[:], in_=x_rows[g][:, t * T : (t + count) * T])
+            windows[g, t] = rows[:]
+            for j in range(1, count):
+                windows[g, t + j] = rows[:, j * T : (j + 1) * T]
 
-        def load_scale_row(i, r):
+        def load_scale_rows(i):
             by_row = (w1_scales, w2_scales)[i].rearrange("g (q r) n -> r q g n", r=4)
-            (nc.scalar, nc.sync)[i].dma_start(out=w_planes[i][8 * i + r : P : 32, :, :].bitcast(I32), in_=by_row[r].bitcast(I32))
+            for r in range(4):
+                (nc.scalar, nc.sync)[i].dma_start(out=w_planes[i][8 * i + r : P : 32, :, :].bitcast(I32), in_=by_row[r].bitcast(I32))
 
         def load_w(i, passes, blocks):
             codes = keep.tile([P, len(passes), len(blocks) * P], U32, name=f"w_codes{i}{passes[0]}{blocks[0]}", align_bytes=64)
@@ -68,17 +73,16 @@ def tile_picked_highway_gelu_l_kernel(
             res_rows[m] = keep.tile([P, T], F32, name=f"res{m}", tag=f"res{m}")
             nc.sync.dma_start(out=res_rows[m][:], in_=res[m * P : (m + 1) * P, :])
 
-        load_x(0, 0)
+        load_x(0, 0, 2)
         nc.sync.dma_start(offsets[:], offs)
-        scale_rows = [(i, r) for i in range(2) for r in range(4)]
-        for i, r in scale_rows[:4]:
-            load_scale_row(i, r)
-        for g, t in ((0, 1), (0, 2), (0, 3), (1, 0), (1, 1), (1, 2)):
-            load_x(g, t)
+        load_scale_rows(0)
+        for t in (2, 3):
+            load_x(0, t, 1)
+        for t in range(3):
+            load_x(1, t, 1)
         load_w(0, (0,), (0, 1))
-        load_x(1, PACK - 1)
-        for i, r in scale_rows[4:]:
-            load_scale_row(i, r)
+        load_x(1, 3, 1)
+        load_scale_rows(1)
         load_w(1, (0,), (0,))
         load_res(0)
         load_w(0, (1,), (0,))
@@ -93,64 +97,98 @@ def tile_picked_highway_gelu_l_kernel(
         nc.gpsimd.memset(zero_in[:], 0.0)
         nc.scalar.activation(out=zero_bias[:], in_=zero_in[:], func=ACT.Gelu_apprx_tanh)
 
-        picked = [keep.tile([P, PACK, S], BF16, name=f"picked{g}", tag=f"picked{g}", align_bytes=64) for g in range(PASSES)]
-        woven, x_codes, x_planes = {}, {}, {}
+        picked = [
+            keep.tile(shape, BF16, name=f"picked{g}", tag=f"picked{g}", align_bytes=64)
+            for g, shape in enumerate(([P, 2, PACK, HALF], [P, PACK, S]))
+        ]
+
+        def picked_at(g, planes, a, b):
+            if g == 1:
+                return picked[1][:, planes, a:b]
+            return picked[0][:, a // HALF, planes, a % HALF : a % HALF + b - a]
+
+        woven = [keep.tile([P, S * PACK], BF16, name=f"woven{g}", tag=f"woven{g}", align_bytes=64) for g in range(PASSES)]
+        slots = [woven[g][:].rearrange("p (c t) -> p c t", t=PACK) for g in range(PASSES)]
+        x_codes, x_planes = {}, {}
 
         def gather_scalar(out_ap, window, offsets_ap):
-            nc.scalar.activation(out=out_ap, in_=window[:].indirect(offsets_ap), func=ACT.Copy)
+            nc.scalar.activation(out=out_ap, in_=window.indirect(offsets_ap), func=ACT.Copy)
 
         def gather_vector(out_ap, window, offsets_ap):
-            nc.vector.tensor_copy(out_ap, window[:].indirect(offsets_ap))
+            nc.vector.tensor_copy(out_ap, window.indirect(offsets_ap))
 
-        def weave(g, h, copy):
-            woven[g, h] = keep.tile([P, HALF * PACK], BF16, name=f"woven{g}{h}", align_bytes=64)
+        def pick(gather, g, t, a, b):
+            gather(picked_at(g, t, a, b), windows[g, t], entries(a, b))
+
+        def pick_both(g, t):
+            gather_vector(picked[g][:, :, t, :], windows[g, t], offsets[:])
+
+        def weave(copy, g, first, last, a, b):
+            h = a // HALF
             copy(
-                out=woven[g, h][:].rearrange("p (c i t) -> p c t i", i=4, t=PACK),
-                in_=picked[g][:, :, halves[h]].rearrange("p t (c i) -> p c t i", i=4),
+                out=slots[g][:, a:b, first:last].rearrange("p (c i) t -> p c t i", i=4),
+                in_=picked[g][:, h, first:last, a - h * HALF : b - h * HALF].rearrange("p t (c i) -> p c t i", i=4),
             )
 
-        def quantise(g, h):
-            x_codes[g, h] = keep.tile([P, HALF], U32, name=f"x_codes{g}{h}", tag=("rows13" if (g, h) == (1, 0) else f"x_codes{g}{h}"), align_bytes=64)
+        def weave_plain(copy, g, first, last, a, b):
+            copy(out=slots[g][:, a:b, first:last], in_=picked_at(g, slice(first, last), a, b).rearrange("p t c -> p c t"))
+
+        def place(g, t, a, b):
+            nc.vector.tensor_copy(out=slots[g][:, a:b, t], in_=picked_at(g, t, a, b))
+
+        def quantise(g, h, tag=None):
+            x_codes[g, h] = keep.tile([P, HALF], U32, name=f"x_codes{g}{h}", tag=tag or f"x_codes{g}{h}", align_bytes=64)
             x_planes[g, h] = keep.tile([P, HALF], U8, name=f"x_planes{g}{h}", align_bytes=64)
-            nc.vector.quantize_mx(out=x_codes[g, h][:].bitcast(FP8X4), scales=x_planes[g, h][:], in_=woven[g, h][:, :])
+            nc.vector.quantize_mx(
+                out=x_codes[g, h][:].bitcast(FP8X4),
+                scales=x_planes[g, h][:],
+                in_=woven[g][:, h * HALF * PACK : (h + 1) * HALF * PACK],
+            )
 
-        def gather_shared(g, t, vector_cuts):
-            for a, b in zip(vector_cuts, vector_cuts[1:]):
-                gather_vector(picked[g][:, t, a:b], rows[g, t], offsets[:, a // 16 : b // 16])
-            cut = vector_cuts[-1]
-            gather_scalar(picked[g][:, t, cut:], rows[g, t], offsets[:, cut // 16 :])
-
-        gather_scalar(picked[0][:, 0, :], rows[0, 0], offsets[:])
-        gather_vector(picked[0][:, 1, :], rows[0, 1], offsets[:])
-        gather_scalar(picked[0][:, 2, :], rows[0, 2], offsets[:])
-        gather_shared(0, 3, (0, HALF))
+        vcopy, scopy = nc.vector.tensor_copy, nc.scalar.copy
         for h in range(2):
-            weave(0, h, nc.vector.tensor_copy)
+            pick(gather_scalar, 0, 0, h * HALF, (h + 1) * HALF)
+        pick_both(0, 1)
+        for h in range(2):
+            pick(gather_scalar, 0, 2, h * HALF, (h + 1) * HALF)
+        pick(gather_vector, 0, 3, 0, HALF)
+        pick(gather_scalar, 0, 3, HALF, S)
+        for h in range(2):
+            weave(vcopy, 0, 0, PACK, h * HALF, (h + 1) * HALF)
         for h in range(2):
             quantise(0, h)
-
-        last = PACK - 1
-        gather_scalar(picked[1][:, 0, :], rows[1, 0], offsets[:])
-        gather_shared(1, 1, (0, 128))
-        gather_shared(1, 2, (0, 96, 192))
-        woven_last = keep.tile([P, S * PACK], BF16, name="woven_last", align_bytes=64)
-        slots = woven_last[:].rearrange("p (c t) -> p c t", t=PACK)
-        for h in range(2):
-            woven[1, h] = woven_last[:, h * HALF * PACK : (h + 1) * HALF * PACK]
-        for copy, cols in (
-            (nc.vector.tensor_copy, slice(0, 96)),
-            (nc.vector.tensor_copy, slice(96, 192)),
-            (nc.vector.tensor_copy, slice(192, SCALAR_WEAVE)),
-            (nc.scalar.copy, slice(SCALAR_WEAVE, S)),
-        ):
-            copy(out=slots[:, cols, 0:last], in_=picked[1][:, 0:last, cols].rearrange("p t c -> p c t"))
-        gather_vector(slots[:, :VECTOR_SHARE, last], rows[1, last], offsets[:, : VECTOR_SHARE // 16])
-        gather_scalar(picked[1][:, last, VECTOR_SHARE:], rows[1, last], offsets[:, VECTOR_SHARE // 16 :])
-        nc.vector.tensor_copy(out=slots[:, VECTOR_SHARE:, last], in_=picked[1][:, last, VECTOR_SHARE:])
-        quantise(1, 0)
+        pick(gather_scalar, 1, 0, 0, S)
+        pick(gather_vector, 1, 1, 0, QUARTER)
+        pick(gather_scalar, 1, 1, QUARTER, S)
+        pick(gather_vector, 1, 2, 0, 96)
+        pick(gather_vector, 1, 2, 96, 192)
+        pick(gather_scalar, 1, 2, 192, S)
+        for a, b in ((0, 96), (96, 192), (192, 448)):
+            weave_plain(vcopy, 1, 0, 3, a, b)
+        weave_plain(scopy, 1, 0, 3, 448, S)
+        gather_vector(slots[1][:, :HALF, 3], windows[1, 3], entries(0, HALF))
+        pick(gather_scalar, 1, 3, HALF, S)
+        place(1, 3, HALF, S)
+        quantise(1, 0, "rows13")
         quantise(1, 1)
 
         sums = {}
+
+        def multiply(i, g, m, h):
+            if g == 0:
+                sums[h, i, m] = (
+                    last_bank[:, :HALF] if (h, i, m) == (1, 1, 1) else psum.tile([P, HALF], F32, name=f"sum{h}{i}{m}")[:]
+                )
+            nc.tensor.matmul_mx(
+                out=sums[h, i, m],
+                lhsT=w_codes[i, g, m].bitcast(FP8X4),
+                lhsT_scale=w_planes[i][8 * i : P, g, m * P : (m + 1) * P],
+                rhs=x_codes[g, h][:].bitcast(FP8X4),
+                rhs_scale=x_planes[g, h][:],
+                start=(g == 0),
+                stop=(g == PASSES - 1),
+            )
+
         last_bank = psum.tile([P, S], F32, name="last_bank")
 
         def warm_up():
@@ -169,44 +207,31 @@ def tile_picked_highway_gelu_l_kernel(
             for i in range(2):
                 for h in range(2):
                     for g in range(PASSES):
-                        if g == 0:
-                            sums[h, i, m] = (
-                                last_bank[:, :HALF] if (h, i, m) == (1, 1, 1) else psum.tile([P, HALF], F32, name=f"sum{h}{i}{m}")[:]
-                            )
-                        cols = slice(m * P, (m + 1) * P)
-                        nc.tensor.matmul_mx(
-                            out=sums[h, i, m],
-                            lhsT=w_codes[i, g, m].bitcast(FP8X4),
-                            lhsT_scale=w_planes[i][8 * i : P, g, cols],
-                            rhs=x_codes[g, h][:].bitcast(FP8X4),
-                            rhs_scale=x_planes[g, h][:],
-                            start=(g == 0),
-                            stop=(g == PASSES - 1),
-                        )
+                        multiply(i, g, m, h)
             if m == 0:
                 warm_up()
 
         passing, y, th, diff, gated, acts = {}, {}, {}, {}, {}, {}
         blocks = [(m, h) for m in range(M_TILES) for h in range(2)]
 
-        def fetch(b, gather):
+        def fetch(b, gather, tag=None):
             m, h = blocks[b]
-            passing[b] = keep.tile([P, HALF], F32, name=f"passing{b}", tag=("picked1" if b == 1 else f"passing{b}"), align_bytes=64)
-            gather(passing[b][:], res_rows[m], half_offsets[h])
+            passing[b] = keep.tile([P, HALF], F32, name=f"passing{b}", tag=tag or f"passing{b}", align_bytes=64)
+            gather(passing[b][:], res_rows[m][:], entries(h * HALF, (h + 1) * HALF))
 
         def activate(b, func):
             m, h = blocks[b]
             if func == ACT.Tanh:
-                th[b] = acts[m][:, 2 + h, :]
+                th[b] = keep.tile([P, HALF], F32, name=f"th{b}")[:]
                 nc.scalar.activation(out=th[b], in_=sums[h, 1, m], func=func, bias=zero_bias[:], scale=0.5)
             else:
-                y[b] = acts[m][:, h, :]
+                y[b] = keep.tile([P, HALF], F32, name=f"y{b}")[:]
                 nc.scalar.activation(out=y[b], in_=sums[h, 0, m], func=func, bias=zero_bias[:])
 
         def subtract(b):
             diff[b] = keep.tile([P, HALF], F32, name=f"diff{b}")
             m, h = blocks[b]
-            looked_up = passing[b][:] if b in passing else res_rows[m][:].indirect(half_offsets[h])
+            looked_up = passing[b][:] if b in passing else res_rows[m][:].indirect(entries(h * HALF, (h + 1) * HALF))
             nc.vector.tensor_tensor(diff[b][:], looked_up, y[b], ALU.subtract)
 
         def gate(b, cols=slice(0, HALF)):
@@ -221,10 +246,9 @@ def tile_picked_highway_gelu_l_kernel(
             nc.sync.dma_start(out=out[m * P : (m + 1) * P, halves[h]][:, cols], in_=result[:])
 
         GELU, TANH = ACT.Gelu_apprx_tanh, ACT.Tanh
-        for m in range(M_TILES):
-            acts[m] = keep.tile([P, 4, HALF], F32, name=f"acts{m}")
+        pieces = (slice(0, HALF // 2), slice(HALF // 2, HALF))
         fetch(0, gather_scalar)
-        fetch(1, gather_vector)
+        fetch(1, gather_vector, "picked1")
         for func in (GELU, TANH):
             for b in (0, 1):
                 activate(b, func)
@@ -233,7 +257,6 @@ def tile_picked_highway_gelu_l_kernel(
         fetch(3, gather_scalar)
         activate(3, GELU)
         activate(3, TANH)
-        pieces = (slice(0, HALF // 2), slice(HALF // 2, HALF))
         subtract(0)
         subtract(1)
         gate(0)

from contextlib import ExitStack

import concourse.mybir as mybir

K, T, S, N = 1024, 1024, 512, 256
FLOPS = 2 * 2 * K * N * S

F32 = mybir.dt.float32
BF16 = mybir.dt.bfloat16
I32 = mybir.dt.int32
U32 = mybir.dt.uint32
U16 = mybir.dt.uint16
U8 = mybir.dt.uint8
FP8X4 = mybir.dt.float8_e4m3fn_x4
ACT = mybir.ActivationFunctionType
ALU = mybir.AluOpType

P = 128
PACK = 4
PASSES = K // (P * PACK)
HALF = S // 2
QUARTER = S // 4
M_TILES = N // P


def tile_picked_highway_gelu_l_kernel(
    tc, xT, res, w1_words, w1_scales, w2_words, w2_scales, offs, out
):
    nc = tc.nc
    with ExitStack() as ctx:
        keep = ctx.enter_context(tc.tile_pool(name="keep", bufs=1))
        psum = ctx.enter_context(tc.psum_pool(name="psum", bufs=1))

        offsets = keep.tile([P, S // 16], U16, name="offsets")
        halves = [slice(h * HALF, (h + 1) * HALF) for h in range(2)]

        def entries(a, b):
            return offsets[:, a // 16 : b // 16]

        x_rows = xT.rearrange("(g p t) c -> g p (t c)", g=PASSES, p=P, t=PACK)
        w_planes = []
        for i in range(2):
            plane = keep.tile([P, PASSES, N], U8, name=f"w_planes{i}", align_bytes=64)
            nc.gpsimd.memset(plane[:].bitcast(I32), 0)
            w_planes.append(plane)

        windows, w_codes, res_rows = {}, {}, {}

        def load_x(g, t, count):
            rows = keep.tile([P, count * T], F32, name=f"rows{g}{t}", tag=f"rows{g}{t}", align_bytes=64)
            nc.sync.dma_start(out=rows[:], in_=x_rows[g][:, t * T : (t + count) * T])
            windows[g, t] = rows[:]
            for j in range(1, count):
                windows[g, t + j] = rows[:, j * T : (j + 1) * T]

        def load_scale_rows(i):
            by_row = (w1_scales, w2_scales)[i].rearrange("g (q r) n -> r q g n", r=4)
            for r in range(4):
                (nc.scalar, nc.sync)[i].dma_start(out=w_planes[i][8 * i + r : P : 32, :, :].bitcast(I32), in_=by_row[r].bitcast(I32))

        def load_w(i, passes, blocks):
            codes = keep.tile([P, len(passes), len(blocks) * P], U32, name=f"w_codes{i}{passes[0]}{blocks[0]}", align_bytes=64)
            by_pass = (w1_words, w2_words)[i].rearrange("g p n t -> p g (n t)").bitcast(I32)
            nc.sync.dma_start(
                out=codes[:].bitcast(I32),
                in_=by_pass[:, passes[0] : passes[-1] + 1, blocks[0] * P : (blocks[-1] + 1) * P],
            )
            for g in passes:
                for m in blocks:
                    w_codes[i, g, m] = codes[:, g - passes[0], (m - blocks[0]) * P : (m - blocks[0] + 1) * P]

        def load_res(m):
            res_rows[m] = keep.tile([P, T], F32, name=f"res{m}", tag=f"res{m}")
            nc.sync.dma_start(out=res_rows[m][:], in_=res[m * P : (m + 1) * P, :])

        load_x(0, 0, 2)
        nc.sync.dma_start(offsets[:], offs)
        load_scale_rows(0)
        for t in (2, 3):
            load_x(0, t, 1)
        for t in range(3):
            load_x(1, t, 1)
        load_w(0, (0,), (0, 1))
        load_x(1, 3, 1)
        load_scale_rows(1)
        load_w(1, (0,), (0,))
        load_res(0)
        load_w(0, (1,), (0,))
        load_w(1, (1,), (0,))
        load_w(0, (1,), (1,))
        load_w(1, (0,), (1,))
        load_res(1)
        load_w(1, (1,), (1,))

        zero_in = keep.tile([P, 1], F32, name="zero_in")
        zero_bias = keep.tile([P, 1], F32, name="zero_bias")
        nc.gpsimd.memset(zero_in[:], 0.0)
        nc.scalar.activation(out=zero_bias[:], in_=zero_in[:], func=ACT.Gelu_apprx_tanh)

        picked = [
            keep.tile(shape, BF16, name=f"picked{g}", tag=f"picked{g}", align_bytes=64)
            for g, shape in enumerate(([P, 2, PACK, HALF], [P, PACK, S]))
        ]

        def picked_at(g, planes, a, b):
            if g == 1:
                return picked[1][:, planes, a:b]
            return picked[0][:, a // HALF, planes, a % HALF : a % HALF + b - a]

        woven = [keep.tile([P, S * PACK], BF16, name=f"woven{g}", tag=f"woven{g}", align_bytes=64) for g in range(PASSES)]
        slots = [woven[g][:].rearrange("p (c t) -> p c t", t=PACK) for g in range(PASSES)]
        x_codes, x_planes = {}, {}

        def gather_scalar(out_ap, window, offsets_ap):
            nc.scalar.activation(out=out_ap, in_=window.indirect(offsets_ap), func=ACT.Copy)

        def gather_vector(out_ap, window, offsets_ap):
            nc.vector.tensor_copy(out_ap, window.indirect(offsets_ap))

        def pick(gather, g, t, a, b):
            gather(picked_at(g, t, a, b), windows[g, t], entries(a, b))

        def pick_both(g, t):
            gather_vector(picked[g][:, :, t, :], windows[g, t], offsets[:])

        def weave(copy, g, first, last, a, b):
            h = a // HALF
            copy(
                out=slots[g][:, a:b, first:last].rearrange("p (c i) t -> p c t i", i=4),
                in_=picked[g][:, h, first:last, a - h * HALF : b - h * HALF].rearrange("p t (c i) -> p c t i", i=4),
            )

        def weave_plain(copy, g, first, last, a, b):
            copy(out=slots[g][:, a:b, first:last], in_=picked_at(g, slice(first, last), a, b).rearrange("p t c -> p c t"))

        def place(g, t, a, b):
            nc.vector.tensor_copy(out=slots[g][:, a:b, t], in_=picked_at(g, t, a, b))

        def quantise(g, h, tag=None):
            x_codes[g, h] = keep.tile([P, HALF], U32, name=f"x_codes{g}{h}", tag=tag or f"x_codes{g}{h}", align_bytes=64)
            x_planes[g, h] = keep.tile([P, HALF], U8, name=f"x_planes{g}{h}", align_bytes=64)
            nc.vector.quantize_mx(
                out=x_codes[g, h][:].bitcast(FP8X4),
                scales=x_planes[g, h][:],
                in_=woven[g][:, h * HALF * PACK : (h + 1) * HALF * PACK],
            )

        vcopy, scopy = nc.vector.tensor_copy, nc.scalar.copy
        for h in range(2):
            pick(gather_scalar, 0, 0, h * HALF, (h + 1) * HALF)
        pick_both(0, 1)
        for h in range(2):
            pick(gather_scalar, 0, 2, h * HALF, (h + 1) * HALF)
        pick(gather_vector, 0, 3, 0, HALF)
        pick(gather_scalar, 0, 3, HALF, S)
        for h in range(2):
            weave(vcopy, 0, 0, PACK, h * HALF, (h + 1) * HALF)
        for h in range(2):
            quantise(0, h)
        pick(gather_scalar, 1, 0, 0, S)
        pick(gather_vector, 1, 1, 0, QUARTER)
        pick(gather_scalar, 1, 1, QUARTER, S)
        pick(gather_vector, 1, 2, 0, 96)
        pick(gather_vector, 1, 2, 96, 192)
        pick(gather_scalar, 1, 2, 192, S)
        for a, b in ((0, 96), (96, 192), (192, 448)):
            weave_plain(vcopy, 1, 0, 3, a, b)
        weave_plain(scopy, 1, 0, 3, 448, S)
        gather_vector(slots[1][:, :HALF, 3], windows[1, 3], entries(0, HALF))
        pick(gather_scalar, 1, 3, HALF, S)
        place(1, 3, HALF, S)
        quantise(1, 0, "rows13")
        quantise(1, 1)

        sums = {}

        def multiply(i, g, m, h):
            if g == 0:
                sums[h, i, m] = (
                    last_bank[:, :HALF] if (h, i, m) == (1, 1, 1) else psum.tile([P, HALF], F32, name=f"sum{h}{i}{m}")[:]
                )
            nc.tensor.matmul_mx(
                out=sums[h, i, m],
                lhsT=w_codes[i, g, m].bitcast(FP8X4),
                lhsT_scale=w_planes[i][8 * i : P, g, m * P : (m + 1) * P],
                rhs=x_codes[g, h][:].bitcast(FP8X4),
                rhs_scale=x_planes[g, h][:],
                start=(g == 0),
                stop=(g == PASSES - 1),
            )

        last_bank = psum.tile([P, S], F32, name="last_bank")

        def warm_up():
            for width in (HALF, HALF // 2):
                nc.tensor.matmul_mx(
                    out=last_bank[:, HALF : HALF + width],
                    lhsT=w_codes[1, 0, 0].bitcast(FP8X4),
                    lhsT_scale=w_planes[1][8:P, 0, :P],
                    rhs=x_codes[0, 1][:, :width].bitcast(FP8X4),
                    rhs_scale=x_planes[0, 1][:, :width],
                    start=True,
                    stop=True,
                )

        for m in range(M_TILES):
            for i in range(2):
                for h in range(2):
                    for g in range(PASSES):
                        multiply(i, g, m, h)
            if m == 0:
                warm_up()

        passing, y, th, diff, gated, acts = {}, {}, {}, {}, {}, {}
        blocks = [(m, h) for m in range(M_TILES) for h in range(2)]

        def fetch(b, gather, tag=None):
            m, h = blocks[b]
            passing[b] = keep.tile([P, HALF], F32, name=f"passing{b}", tag=tag or f"passing{b}", align_bytes=64)
            gather(passing[b][:], res_rows[m][:], entries(h * HALF, (h + 1) * HALF))

        def activate(b, func):
            m, h = blocks[b]
            if func == ACT.Tanh:
                th[b] = keep.tile([P, HALF], F32, name=f"th{b}")[:]
                nc.scalar.activation(out=th[b], in_=sums[h, 1, m], func=func, bias=zero_bias[:], scale=0.5)
            else:
                y[b] = keep.tile([P, HALF], F32, name=f"y{b}")[:]
                nc.scalar.activation(out=y[b], in_=sums[h, 0, m], func=func, bias=zero_bias[:])

        def subtract(b):
            diff[b] = keep.tile([P, HALF], F32, name=f"diff{b}")
            m, h = blocks[b]
            looked_up = passing[b][:] if b in passing else res_rows[m][:].indirect(entries(h * HALF, (h + 1) * HALF))
            nc.vector.tensor_tensor(diff[b][:], looked_up, y[b], ALU.subtract)

        def gate(b, cols=slice(0, HALF)):
            if b not in gated:
                gated[b] = keep.tile([P, HALF], F32, name=f"gated{b}")
            nc.vector.scalar_tensor_tensor(gated[b][:, cols], th[b][:, cols], 1.0, diff[b][:, cols], ALU.subtract, ALU.mult)

        def finish(b, cols=slice(0, HALF)):
            m, h = blocks[b]
            result = keep.tile([P, cols.stop - cols.start], F32, name=f"result{b}{cols.start}")
            nc.vector.scalar_tensor_tensor(result[:], gated[b][:, cols], -0.5, y[b][:, cols], ALU.mult, ALU.add)
            nc.sync.dma_start(out=out[m * P : (m + 1) * P, halves[h]][:, cols], in_=result[:])

        GELU, TANH = ACT.Gelu_apprx_tanh, ACT.Tanh
        pieces = (slice(0, HALF // 2), slice(HALF // 2, HALF))
        fetch(0, gather_scalar)
        fetch(1, gather_vector, "picked1")
        for func in (GELU, TANH):
            for b in (0, 1):
                activate(b, func)
        activate(2, GELU)
        activate(2, TANH)
        fetch(3, gather_scalar)
        activate(3, GELU)
        activate(3, TANH)
        subtract(0)
        subtract(1)
        gate(0)
        gate(1)
        finish(0)
        subtract(2)
        finish(1)
        gate(2)
        subtract(3)
        finish(2)
        for cols in pieces:
            gate(3, cols)
        for cols in pieces:
            finish(3, cols)
